import numpy as np, ml_dtypes
CORES = [48,51,52,55]
N = 4
BF = ml_dtypes.bfloat16
def gentries(a):
    return np.ascontiguousarray(a.reshape(8, 16, -1).transpose(0, 2, 1)).reshape(8, -1)
def gtable(e):
    e = np.asarray(e); return np.ascontiguousarray(e.reshape(8, -1, 16).transpose(0, 2, 1)).reshape(128, -1).astype(np.int32)
W, C, S, F, HOPS, PH = 8192, 256, 8, 320, 3, 4
R = S * C
def lengths(rng, even):
    return 2 + rng.multinomial(W - F - 2 * C, rng.dirichlet(np.full(C, even)))
def short(rng):
    ln = 2 + (rng.random(C) < 0.3).astype(np.int64); ln[rng.integers(0, C)] += W - F - int(np.sum(ln)); return ln
def near(a, k):
    o, s, at, ln = a
    return o[s + (at + k) % ln]
def away(rng, a):
    return np.roll(near(a, rng.integers(0, W, (S, C))), C // 2, axis=1)
def store(rng, ln, o):
    s = F + np.concatenate([np.zeros(1, np.int64), np.add.accumulate(ln)[:-1]]); who = np.repeat(np.arange(C), ln)
    m = rng.integers(0, W, W); i = np.arange(F, W)
    m[o[F:]] = o[s[who] + (i - s[who] + 1) % ln[who]]
    return m, (o, s, np.minimum((rng.random(C) * ln).astype(np.int64), ln - 1), ln)
def put(o, i, v):
    j = int(np.flatnonzero(o == v)[0]); o[j] = o[i]; o[i] = v
def parts(rng, even=(0.5, 2.0, 20.0), share=0.6, ends=False):
    x = rng.integers(0, 16, (N, 8, 16, W), dtype=np.int32); q = rng.integers(0, 16, (N, 8, 16, R), dtype=np.int32); th = rng.integers(50, 90, (N, 8, R))
    nx = np.zeros((N, 8, W), np.int64); fr = np.zeros((N, 8, F), np.int64); cu = np.zeros((N, 8, C), np.int64); pin = np.zeros((N, 8, R), np.int64); a = {}
    for r in range(N):
        for g in range(8):
            o = rng.permutation(W)
            if ends and g % 4 == 0: put(o, 0, 0); put(o, F - 1, W - 1)
            if ends and g % 4 == 1: put(o, F, 0); put(o, F + 1, W - 1)
            if ends and g % 4 == 2: put(o, 0, W - 1); put(o, W - 1, 0)
            ln = short(rng) if ends else lengths(rng, float(rng.choice(np.array(even))))
            nx[r, g], s = store(rng, ln, o); a[r, g] = s
            fr[r, g] = o[:F]; cu[r, g] = near(s, 0)
            close = rng.random((S, C)) < share * rng.random((1, C))
            pin[r, g] = np.where(close, near(s, rng.integers(-5, 2, (S, C))), rng.integers(0, W, (S, C))).reshape(R)
    return x, nx, fr, cu, q, pin, th, a
def pack(x, nx, fr, cu, q, pin, th):
    return {"x": x.reshape(N, 128, W).astype(np.float32).astype(BF), "nx": nx.astype(np.int32), "fr": fr.astype(np.int32), "cu": np.stack([gtable(v) for v in cu]),
            "q": q.reshape(N, 128, R).astype(np.float32).astype(BF), "pin": np.stack([gtable(v) for v in pin]), "th": np.stack([gtable(v) for v in th])}
def setup_inputs(rng):
    x, nx, fr, cu, q, pin, th, a = parts(rng)
    return pack(x, nx, fr, cu, q, pin, th)
def setup_inputs_alike(rng):
    x, nx, fr, cu, q, pin, th, a = parts(rng)
    for r in range(N):
        for g in range(8):
            s = a[r, g]
            if g % 2 == 0:
                pin[r, g] = rng.choice(np.array([0, W - 1, near(s, 0)[0], near(s, 1)[1]]), R); q[r, g] = q[r, g][:, rng.integers(0, 2, R)]
            else:
                pin[r, g] = np.tile(np.roll(near(s, 0), -1), S); q[r, g] = np.tile(x[r, g][:, np.roll(near(s, 1), -1)], (1, S)); th[:, g] = 0
    return pack(x, nx, fr, cu, q, pin, th)
def setup_inputs_dry(rng):
    x, nx, fr, cu, q, pin, th, a = parts(rng)
    x[:, 4] = rng.integers(0, 16, (N, 16, 1))
    for g in (5, 6):
        x[:, g] = rng.integers(0, 2, (N, 16, 1)); q[:, g] = rng.integers(14, 16, (N, 16, R))
    m = min(C, F); L = F - m; d = C // 8
    for r in range(N):
        for g in range(8):
            s = a[r, g]; p = away(rng, s); T = np.full((S, C), 255); one = near(s, 1)
            if g in (0, 2):
                p = np.array(pin[r, g]).reshape(S, C); p[0] = near(s, 0); p[1] = near(s, 0); T = np.zeros((S, C), np.int64)
                q[r, g, :, :C] = x[r, g][:, one]; q[r, g, :, C:2 * C] = x[r, g][:, near(s, 2)]
            elif g == 4:
                p[0] = near(s, 0); w = rng.permutation(m); u = fr[r, g][rng.permutation(m)]; h = L + m // 2
                nx[r, g, u[:L]] = fr[r, g, m:]; nx[r, g, fr[r, g, m:]] = one[w[:L]]; p[1, w[:L]] = u[:L]; T[1, w[:L]] = 0
                nx[r, g, u[L:h]] = one[w[L:h]]; p[0, w[L:h]] = u[L:h]
            elif g == 5:
                e = m - d; b = L + d; k = int(rng.integers(1, 16)) if r % 2 == 0 else int(rng.integers(16, 48))
                p[0, :e] = near(s, 0)[:e]; T[0, :d] = 0; T[0, d:e] = 80; T[0, b + rng.permutation(e - b)[:k]] = 255
            elif g == 6:
                p[0] = one; T = rng.integers(150, 241, (S, C))
            pin[r, g] = p.reshape(R); th[(r + 1) % N, g] = T.reshape(R)
    return pack(x, nx, fr, cu, q, pin, th)
def setup_inputs_short(rng):
    x, nx, fr, cu, q, pin, th, a = parts(rng, ends=True); th = rng.integers(20, 130, (N, 8, R))
    for r in range(N):
        for g in range(8):
            s = a[r, g]; p = near(s, rng.integers(-2, 2, (S, C))).reshape(R)
            p = np.where(rng.random(R) < 0.25, fr[r, g][rng.integers(0, F, R)], p)
            pin[r, g] = np.where(rng.random(R) < 0.3, rng.integers(0, W, R), p)
            if g < 4: nx[r, g, fr[r, g]] = fr[r, g]
            if g == 7:
                e = np.flatnonzero((s[3] <= HOPS) & (rng.random(C) < 0.5)); v = near(s, 1)[e]; j = (C * np.arange(S)[:, None] + e[None, :]).reshape(-1)
                pin[r, g, j] = np.tile(v, S); q[r, g][:, j] = np.tile(x[r, g][:, v], (1, S)); th[(r + 1) % N, g, j] = 0
    return pack(x, nx, fr, cu, q, pin, th)
def setup_inputs_ties(rng):
    x, nx, fr, cu, q, pin, th, a = parts(rng, share=1.0)
    x[:, ::2] = rng.choice(np.array([2, 5, 6, 9]), (N, 4, 1, W)); q[:, ::2] = rng.integers(1, 11, (N, 4, 1, R)); th[:, ::2] = 16 * rng.integers(0, 5, (N, 4, R))
    x[:, 1::2] = rng.integers(0, 2, (N, 4, 16, W)); q[:, 1::2] = rng.integers(0, 2, (N, 4, 16, R)); th[:, 1::2] = rng.integers(2, 9, (N, 4, R))
    return pack(x, nx, fr, cu, q, pin, th)
def setup_inputs_spread(rng):
    x, nx, fr, cu, q, pin, th, a = parts(rng, even=(0.1, 0.3))
    x = np.minimum((16 * rng.random((N, 8, 16, W)) ** np.exp2(rng.integers(-2, 4, (N, 8, 1, W)))).astype(np.int32), 15)
    q = np.minimum((16 * rng.random((N, 8, 16, R)) ** np.exp2(rng.integers(-2, 4, (N, 8, 1, R)))).astype(np.int32), 15)
    return pack(x, nx, fr, cu, q, pin, rng.integers(0, 160, (N, 8, R)))
def check_inputs(d):
    bad = []
    for k in ("x", "q"):
        v = np.asarray(d[k]).astype(np.float32)
        if not np.all((v >= 0) & (v <= 15) & (v == np.floor(v))): bad.append("whole numbers of " + k)
    for k, hi in (("nx", W - 1), ("fr", W - 1), ("cu", W - 1), ("pin", W - 1), ("th", 255)):
        if np.min(d[k]) < 0 or np.max(d[k]) > hi: bad.append("range of " + k)
    if bad: return bad
    for r in range(N):
        cl = gentries(np.asarray(d["cu"][r])).astype(np.int64)
        for g in range(8):
            f = np.asarray(d["fr"][r][g]).astype(np.int64); m = np.asarray(d["nx"][r][g]).astype(np.int64)
            if len(np.unique(f)) != F:
                bad.append("different numbers of fr"); continue
            live = np.ones(W, bool); live[f] = False; ids = np.flatnonzero(live)
            if not np.array_equal(np.sort(m[ids]), ids) or np.any(m[ids] == ids):
                bad.append("rings of nx"); continue
            jump = np.where(live, m, np.arange(W)); lab = np.arange(W)
            for _ in range(W.bit_length()): lab = np.minimum(lab, lab[jump]); jump = jump[jump]
            if not np.all(live[cl[g]]) or not np.array_equal(np.sort(lab[cl[g]]), np.unique(lab[ids])): bad.append("one cursor in each ring")
    return sorted(set(bad))
def reference(x, nx, fr, cu, q, pin, th):
    X = x.astype(np.float32).astype(np.int32).reshape(N, 8, 16, W); Q = q.astype(np.float32).astype(np.int32).reshape(N, 8, 16, R); M = nx.astype(np.int64)
    c = np.stack([gentries(v) for v in cu]).astype(np.int64); P = np.stack([gentries(v) for v in pin]).astype(np.int64); t = np.stack([gentries(v) for v in th]).astype(np.int64)
    free = {(r, g): fr[r, g].astype(np.int64) for r in range(N) for g in range(8)}
    num = {k: np.zeros(0, np.int64) for k in free}; ring = {k: np.zeros(0, np.int64) for k in free}
    for phase in range(PH):
        n = P; old = P
        for h in range(HOPS):
            n = np.take_along_axis(M, n, 2); xn = np.take_along_axis(X, n[:, :, None, :], 3)
            d = np.add.reduce(np.abs(xn - Q), axis=2)
            if h == 0: least, at, xp = d, n, xn
            else:
                less = d < least
                least = np.where(less, d, least); at = np.where(less, n, at); xp = np.where(less[:, :, None, :], xn, xp)
        P = at; Q = (Q + xp) >> 1
        stay = np.roll(least >= t, -1, axis=0)
        for r, g in free:
            fl = free[r, g]; m = min(C, len(fl)); f = fl[:m]; a = c[r, g, :m].copy(); b = M[r, g, a]
            X[r, g][:, f] = (X[r, g][:, b] + X[r, g][:, a]) >> 1
            M[r, g, f] = M[r, g, b]; M[r, g, a] = f; c[r, g, :m] = f
            v = np.concatenate([num[r, g], b]); w = np.concatenate([ring[r, g], np.arange(m)])
            new4, old4, bit4 = P[r, g].reshape(S, C)[:, w], old[r, g].reshape(S, C)[:, w], stay[r, g].reshape(S, C)[:, w]
            held = np.any((new4 == v) | ((old4 == v) & bit4), axis=0)
            free[r, g] = np.concatenate([fl[m:], v[~held]]); num[r, g] = v[held]; ring[r, g] = w[held]
        if phase < PH - 1: Q = np.roll(Q, 1, axis=0)
    return {"yq": Q.reshape(N, 128, R).astype(np.float32).astype(BF), "yp": np.stack([gtable(v) for v in P]).astype(np.float32), "yn": M.astype(np.float32)}

@@ -1,0 +1,576 @@
+import math
+import numpy as np
+from concourse.bass import DstId, RemoteDMATransfer
+from concourse.mybir import AluOpType as ALU, ActivationFunctionType as ACT
+
+W, C, R, PH = 8192, 256, 2048, 4
+NCH = 2
+CS = R // NCH
+CW = CS // 16
+WT = W + 512
+ZW = 144
+Z_ID, Z_K1, Z_K2, Z_K3, Z_L3, Z_L2, Z_L1, Z_A, Z_Q, Z_M, Z_S = range(11)
+NZ = 11
+FLW = 2432
+A_OFF = [241.0, 177.0, 145.0, 129.0]
+C_OFF = 112.5
+OPT = {"neg0": {(3, 0), (3, 1)}, "pre": 1, "fill": 3, "iters": 90000, "seed": 1}
+
+BF, F32, I32, U16 = "bfloat16", "float32", "int32", "uint16"
+SCRATCH = {name: ("sbuf", [128, n], dtype) for name, n, dtype in (
+    ("X", WT, BF), ("TB", WT, BF), ("TO", WT, BF), ("ZB", NZ * ZW, BF),
+    ("MI", 128, BF), ("MPc", 128, BF), ("MPm", 128, BF), ("MPn", 128, BF), ("MPf", 128, BF), ("MBN", 256, BF),
+    ("NXI", 512, I32), ("NXH", 512, BF), ("NXL", 512, BF), ("IDA", 512, BF), ("IDH", 512, BF), ("IDL", 512, BF), ("SXS", 512, BF),
+    ("FI0", 80, I32), ("FI1", 80, I32), ("FI", 80, I32), ("FH", 80, BF), ("FL", 80, BF), ("FLB", FLW, BF),
+    ("PI0", 8, I32), ("PI1", 8, I32), ("RC", 8, F32), ("RD", 8, F32), ("I16", 48, F32), ("TT", 48, F32), ("REP", 16, U16),
+    ("PIN", 128, I32), ("THI", 128, I32), ("TH", 128, BF), ("CUI", 16, I32),
+    ("LP", 128 * (PH + 1), U16), ("LN", 128 * 3, U16), ("G", 4 * R, BF), ("MN", 3 * R, BF), ("DF", 3 * R, BF),
+    ("QR", PH * R, BF), ("V", PH * R, BF), ("XG", PH * R, BF), ("QF", CS, F32), ("YQ", R, BF),
+    ("K1S", 128, F32), ("M1", 128, F32), ("M2", 128, I32), ("A", 256 * PH, I32), ("WS", 128 * 3, BF), ("WL", 128 * 3, BF),
+    ("YP", 128, F32), ("LW", 64 * PH + 16, U16), ("FW", 64 * PH + 16, F32), ("F2", 16, F32), ("C1", 16, F32), ("T1", 16, F32),
+    ("H", 16 * PH, BF), ("GC", 256, BF), ("GN", 256 * PH, BF), ("XCN", 512, BF), ("XF", 256, BF), ("M192", 256, BF),
+    ("NCS", 512, BF), ("E", 768, BF), ("U", 48 * 3, BF), ("S", 48, BF), ("TM", 48, F32), ("TG", 48, U16), ("BC", 24, F32))}
+SCRATCH.update({name: ("psum", [128, 512], F32) for name in ("PL0", "PL1", "PA0", "PA1", "PB0", "PB1", "PW", "PN")})
+SEMAPHORES = (["ev", "ea", "ep", "eg"] + ["d%d" % i for i in range(40)]
+              + ["arr%d" % i for i in range(10)] + ["out%d" % i for i in range(10)])
+
+GUESS = [(1.0, 1.5, 3.5, 0.55, 60.0, 120.0, 200.0, 1800.0, 2000.0),
+         (1.0, 1.1, 5.0, 0.45, 50.0, 200.0, 300.0, 1500.0, 4000.0),
+         (1.1, 2.0, 2.0, 0.80, 60.0, 80.0, 150.0, 2000.0, 2000.0),
+         (1.0, 1.5, 3.8, 0.45, 60.0, 250.0, 350.0, 2200.0, 3000.0)]
+
+
+def plan(T, nxt, prv):
+    ops = []
+    cnt = {"d": 0, "r": 0}
+
+    def add(eng, fn, rd, wr, cost, kind="c", sem=None, n=1, after=None, nbytes=0):
+        ops.append({"eng": eng, "fn": fn, "rd": rd, "wr": wr, "cost": cost, "kind": kind, "sem": sem, "n": n,
+                    "after": after, "bytes": nbytes})
+        return len(ops) - 1
+
+    def ap(r):
+        return T[r[0]][:, r[1]:r[2]] if len(r) == 3 else T[r[0]][:, r[1]:r[2]:r[3]]
+
+    def width(r):
+        return r[2] - r[1] if len(r) == 3 else len(range(r[1], r[2], r[3]))
+
+    def two(*rs):
+        return all(SCRATCH[r[0]][2] in (BF, U16) for r in rs)
+
+    def ind(win, lst):
+        return ap(win).indirect(ap(lst))
+
+    def cy(n, c):
+        return ("c", max(64, n * c))
+
+    def dma(eng, out, in_, rd, wr, nbytes, after=None, **kw):
+        s = "d%d" % cnt["d"]
+        cnt["d"] += 1
+        return add(eng, lambda q: q.dma_start(out, in_, **kw), rd, wr, ("n", 1000.0 if eng == "g" else 60.0), "dma", s, 16, after, nbytes)
+
+    def memset(o, v):
+        add("v", lambda q: q.memset(ap(o), v), [], [o], cy(width(o), 0.5 if two(o) else 1))
+
+    def copy(o, i):
+        add("v", lambda q: q.tensor_copy(ap(o), ap(i)), [i], [o], cy(width(o), 0.5 if two(o, i) else 1))
+
+    def tt(o, a, b, op):
+        ps = SCRATCH[a[0]][0] == "psum" or SCRATCH[b[0]][0] == "psum"
+        add("v", lambda q: q.tensor_tensor(ap(o), ap(a), ap(b), op), [a, b], [o], cy(width(o), 1 if ps else 2))
+
+    def ts(o, i, s1, s2, op0, op1=None):
+        rd = [i] + [s for s in (s1, s2) if isinstance(s, tuple)]
+        a1 = ap(s1) if isinstance(s1, tuple) else s1
+        a2 = ap(s2) if isinstance(s2, tuple) else s2
+        if op1 is None:
+            fn = lambda q: q.tensor_scalar(ap(o), ap(i), a1, None, op0)
+        else:
+            fn = lambda q: q.tensor_scalar(ap(o), ap(i), a1, a2, op0, op1)
+        add("v", fn, rd, [o], cy(width(o), 0.5 if two(o, i) else 1))
+
+    def gtt(o, win, lst, b, op):
+        add("v", lambda q: q.tensor_tensor(ap(o), ind(win, lst), ap(b), op), [win, lst, b], [o], ("g", width(o)))
+
+    def scatter(win, lst, src, more=None):
+        if more is None:
+            add("v", lambda q: q.tensor_copy(ind(win, lst), ap(src)), [lst, src], [win], ("s", width(src)))
+        else:
+            add("v", lambda q: q.tensor_tensor(ind(win, lst), ap(src), ap(more), ALU.add), [lst, src, more], [win], ("s", width(src)))
+
+    def act(o, i, func=ACT.Identity, bias=0.0, scale=1.0):
+        return add("a", lambda q: q.activation(ap(o), ap(i), func, bias, scale), [i], [o], cy(width(o), 1))
+
+    def gact(o, win, lst, bias=0.0, scale=1.0):
+        add("a", lambda q: q.activation(ap(o), ind(win, lst), ACT.Identity, bias, scale), [win, lst], [o], ("g", width(o)))
+
+    def mm(o, terms):
+        def fn(q):
+            ins = None
+            for k, (l, r) in enumerate(terms):
+                ins = q.matmul(ap(o), ap(l), ap(r), k == 0, k == len(terms) - 1)
+            return ins
+        rd = []
+        for l, r in terms:
+            rd += [l, r]
+        add("p", fn, rd, [o], ("p", len(terms) * max(64, width(o))))
+
+    def z(s, i):
+        return ("ZB", s * ZW + 15 - i, s * ZW + 143 - i)
+
+    def wrap(s, name, c0, n):
+        return [(z(s, i), (name, c0 + i, c0 + n, 16)) for i in range(16)]
+
+    def sel(o, pattern, op, fill, base, cm):
+        return add("g", lambda q: q.affine_select(ap(o), ap(o), pattern, op, fill, base, cm), [o], [o], ("n", 200.0 + 2 * width(o)))
+
+    def iota(o, pattern, base, cm):
+        if SCRATCH[o[0]][2] == I32:
+            fn = lambda q: q.iota(ap(o), pattern, base, cm)
+        else:
+            fn = lambda q: q.iota(ap(o), pattern, base, cm, allow_small_or_imprecise_dtypes=True)
+        add("g", fn, [], [o], ("n", 160.0 + 2 * width(o)))
+
+    def send(srcs, dst, to, after=None):
+        k = cnt["r"]
+        cnt["r"] += 1
+        rid, pid, mask, ne = to
+        arr, out = "arr%d" % k, "out%d" % k
+        if len(srcs) == 1:
+            fn = lambda q: q.remote_dma(ap(dst), ap(srcs[0]), T.sem[arr], T.sem[out], pid, rid, mask)
+        else:
+            fn = lambda q: q.remote_dma_fused([RemoteDMATransfer(
+                dst_ids=[DstId(rid=rid, pnc=pid)], dma_engine_mask=mask, remote_sem=T.sem[arr],
+                srcs=[ap(s) for s in srcs], dsts=[ap(dst)], alu_op=1)], local_sem=T.sem[out])
+        i = add("g", fn, list(srcs), [], ("n", 600.0 if k else 2000.0), "send", out, ne, after, 256 * width(dst) * len(srcs))
+        add("n", None, [], [dst], ("n", 0.0), "arrive", arr, ne, after=i)
+        return i
+
+    XW, TW = ("X", 0, W), ("TB", 0, W)
+    MI = ("MI", 0, 128)
+
+    def load(name, src, c0, c1, after):
+        return dma("s", T[name][:, c0:c1], src[:, c0:c1], [], [(name, c0, c1)], 256 * (c1 - c0), after)
+    i = dma("s", T.NXI[:], T.nx[:], [], [("NXI", 0, 512)], 1 << 18)
+    j = dma("a", T.PIN[:], T.pin[:], [], [("PIN", 0, 128)], 1 << 16)
+    for k in range(OPT["pre"]):
+        i = load("X", T.x, 2048 * k, 2048 * (k + 1), i)
+    fill = OPT["fill"]
+    memset(("TB", 0, 1024), 1.0)
+    for k in range(fill):
+        ops[act(("TB", 1024 * (k + 1), 1024 * (k + 2)), ("TB", 0, 1024))]["after"] = j
+    memset(("TB", 1024 * (fill + 1), W), 1.0)
+    memset(("ZB", Z_L3 * ZW, Z_A * ZW), 0.0)
+    memset(("ZB", 0, Z_L3 * ZW), 0.0)
+    memset(("ZB", Z_A * ZW, NZ * ZW), 0.0)
+    copy(("NXH", 0, 512), ("NXI", 0, 512))
+    tt(("NXL", 0, 512), ("NXI", 0, 512), ("NXH", 0, 512), ALU.subtract)
+    i = dma("s", T.TB[0:128:16, 0:W], T.NXH[:], [("NXH", 0, 512)], [("TBm", 0, W)], 1 << 17, i)
+    i = dma("s", T.TB[1:128:16, 0:W], T.NXL[:], [("NXL", 0, 512)], [("TBm", 0, W)], 1 << 17, i)
+    i = load("QR", T.q, 0, CS, i)
+    for k in range(OPT["pre"], 4):
+        i = load("X", T.x, 2048 * k, 2048 * (k + 1), i)
+    i = load("QR", T.q, CS, R, i)
+    i = dma("s", T.THI[:], T.th[:], [], [("THI", 0, 128)], 1 << 16, i)
+    copy(("LP", 0, 128), ("PIN", 0, 128))
+
+    def zrow(s0, s1, r, v):
+        return sel(("ZB", s0 * ZW + 15, s1 * ZW, 16), [[0, s1 - s0], [-16, 9]], ALU.not_equal, v, -r, 1)
+    zrow(Z_L3, Z_L1 + 1, 0, 1.0)
+    j = zrow(Z_L3, Z_L1 + 1, 1, 1.0)
+    dma("g", T.CUI[:], T.cu[:], [], [("CUI", 0, 16)], 1 << 13, j)
+    zrow(Z_L2, Z_L2 + 1, 5, 8192.0)
+    zrow(Z_K3, Z_L3 + 1, 5, 16384.0)
+    zrow(Z_K2, Z_K2 + 1, 5, 8192.0)
+    zrow(Z_ID, Z_K3 + 1, 3, 1.0)
+    zrow(Z_ID, Z_K3 + 1, 4, 1.0)
+    zrow(Z_K1, Z_K3 + 1, 2, 32768.0)
+    for s, v in ((Z_A, 32768.0), (Z_Q, -32768.0), (Z_M, -65536.0), (Z_S, 1.0)):
+        memset(("ZB", s * ZW + 15, (s + 1) * ZW, 16), v)
+    zb = ("ZB", Z_A * ZW + 15, NZ * ZW, 16)
+    sel(zb, [[0, 4], [-16, 9]], ALU.is_ge, 0.0, 0, 1)
+    sel(zb, [[0, 4], [16, 9]], ALU.is_ge, 0.0, 15, -1)
+    memset(MI, 1.0)
+    sel(MI, [[-1, 128]], ALU.is_equal, 0.0, 0, 1)
+    memset(("MBN", 0, 128), 1.0)
+    memset(("MBN", 128, 256), -1.0)
+    sel(("MBN", 0, 256), [[0, 2], [-16, 8], [0, 16]], ALU.is_ge, 0.0, 0, 1)
+    sel(("MBN", 0, 256), [[0, 2], [16, 8], [0, 16]], ALU.is_ge, 0.0, 15, -1)
+    sel(("MBN", 128, 256), [[-1, 128]], ALU.is_ge, 0.0, 0, 1)
+    sel(("MBN", 128, 256), [[-1, 128]], ALU.not_equal, -4096.0, 0, 1)
+    for name, pairs in (("MPc", ((2, 2, 1.0), (3, 3, 1.0), (4, 4, 1.0), (5, 5, 1.0))), ("MPm", ((0, 3, 1.0), (1, 4, 1.0))),
+                        ("MPn", ((0, 0, 1.0), (1, 1, 1.0), (5, 5, 1.0), (2, 5, -3072.0))), ("MPf", ((3, 3, 1.0), (4, 4, 1.0)))):
+        memset((name, 0, 128), 0.0)
+        for dst, src, v in pairs:
+            sel((name, dst, 128, 16), [[-16, 8]], ALU.not_equal, v, -src, 1)
+
+    iota(("PI0", 0, 1), [[0, 1]], 0, 1)
+    ts(("PI1", 0, 1), ("PI0", 0, 1), 15, None, ALU.bitwise_and)
+    copy(("RC", 0, 1), ("PI1", 0, 1))
+    ts(("RD", 0, 1), ("PI1", 0, 1), 512.0, None, ALU.mult)
+    iota(("I16", 0, 48), [[16, 48]], 832 - 4095, 0)
+    ts(("TT", 0, 48), ("I16", 0, 48), ("RC", 0, 1), None, ALU.add)
+    ts(("REP", 0, 16), ("I16", 0, 16), 0.0, ("RC", 0, 1), ALU.mult, ALU.add)
+    iota(("IDL", 0, 512), [[0, 8], [1, 64]], 0, 0)
+    iota(("IDA", 0, 512), [[64, 8], [0, 64]], 0, 0)
+    ts(("IDH", 0, 512), ("IDA", 0, 512), ("RD", 0, 1), None, ALU.add)
+    iota(("FI0", 0, 80), [[1, 80]], 0, 80)
+    ts(("FI1", 0, 80), ("FI0", 0, 80), 255, None, ALU.bitwise_and)
+    ts(("FI", 0, 80), ("FI1", 0, 80), float(W), None, ALU.add)
+    for k in range(4):
+        dma("s", T.FI[k:128:16, 0:80], T.fr[:, 80 * k:80 * (k + 1)], [], [("FIm", 0, 80)], 2560, i)
+    copy(("FH", 0, 80), ("FI", 0, 80))
+    tt(("FL", 0, 80), ("FI", 0, 80), ("FH", 0, 80), ALU.subtract)
+    memset(("FLB", 0, 1024), 0.0)
+    dma("s", T.FLB[3:128:16, 0:1280], T.FH[:], [("FH", 0, 80)], [("FLBm", 0, FLW)], 20480)
+    dma("s", T.FLB[4:128:16, 0:1280], T.FL[:], [("FL", 0, 80)], [("FLBm", 0, FLW)], 20480)
+    ts(("TH", 0, 128), ("THI", 0, 128), 32768.0, None, ALU.mult)
+    copy(("LW", 0, 16), ("CUI", 0, 16))
+    copy(("FW", 0, 16), ("CUI", 0, 16))
+    memset(("H", 0, 16), 16384.0)
+    memset(("M192", 0, 256), -192.0)
+    memset(("BC", 0, 1), 64.0 + 256.0 + 4095.0)
+    for a in range(NCH):
+        ts(("V", a * CS, (a + 1) * CS), ("QR", a * CS, (a + 1) * CS), A_OFF[0], None, ALU.add)
+    mm(("PN", 0, 512), [(z(Z_S, k), ("X", 512 * k, 512 * (k + 1))) for k in range(16)])
+    act(("SXS", 0, 512), ("PN", 0, 512))
+
+    for p in range(PH):
+        last = p == PH - 1
+
+        def lst(h, a):
+            return ("LP", 128 * p + CW * a, 128 * p + CW * (a + 1)) if h == 0 else ("LN", 128 * (h - 1) + CW * a, 128 * (h - 1) + CW * (a + 1))
+
+        def run(name, a, k=p):
+            return (name, k * R + a * CS, k * R + (a + 1) * CS)
+
+        if p > 0:
+            for a in range(NCH):
+                ts(run("QR", a), run("V", a), 0.5 ** p, -A_OFF[p], ALU.mult, ALU.add)
+        if last:
+            act(("QF", 0, CS), run("QR", NCH - 1), ACT.Identity, 257.5)
+        for h in range(4):
+            for a in range(NCH):
+                if h < 3 or p > 0:
+                    gact(run("G", a, h), TW, lst(h, a))
+                if h < 3:
+                    mm(("PL%d" % a, 0, CW), wrap(Z_L1, "G", h * R + a * CS, CS))
+                    copy(lst(h + 1, a), ("PL%d" % a, 0, CW))
+            for a in range(NCH):
+                if h == 0:
+                    if not last:
+                        terms = [(MI, ("TH", CW * a, CW * (a + 1)))]
+                        if p > 0:
+                            terms += wrap(Z_Q, "QR", p * R + a * CS, CS)
+                        mm(("PB%d" % a, 128, 128 + CW), terms)
+                    continue
+                m0 = (h - 1) * R + a * CS
+                mn, df = run("MN", a, h - 1), run("DF", a, h - 1)
+                if p == 0:
+                    gtt(df, XW, lst(h, a), run("QR", a), ALU.subtract)
+                    terms = wrap((Z_L1, Z_L2, Z_L3)[h - 1], "G", m0, CS)
+                    if (h, a) in OPT["neg0"]:
+                        ts(mn, df, 0.0, None, ALU.min)
+                        terms += wrap(Z_A, "DF", m0, CS) + wrap(Z_M, "MN", m0, CS)
+                    else:
+                        act(mn, df, ACT.Abs)
+                        terms += wrap(Z_A, "MN", m0, CS)
+                else:
+                    gtt(mn, XW, lst(h, a), run("QR", a), ALU.min)
+                    terms = wrap((Z_K1, Z_K2, Z_K3)[h - 1], "G", h * R + a * CS, CS) + wrap(Z_M, "MN", m0, CS)
+                cw = (CW * a, CW * (a + 1))
+                if h == 1:
+                    mm(("PA%d" % a, 0, CW), terms)
+                    act(("K1S",) + cw, ("PA%d" % a, 0, CW))
+                    continue
+                if h == 2:
+                    mm(("PA%d" % a, 128, 128 + CW), terms)
+                    tt(("M1",) + cw, ("K1S",) + cw, ("PA%d" % a, 128, 128 + CW), ALU.min)
+                    continue
+                mm(("PB%d" % a, 0, CW), terms)
+                tt(("M2",) + cw, ("M1",) + cw, ("PB%d" % a, 0, CW), ALU.min)
+                pn = ("A", 256 * p + cw[0], 256 * p + cw[1])
+                ts(pn, ("M2",) + cw, W - 1, None, ALU.bitwise_and)
+                l0 = 128 * (p + 1) + cw[0]
+                copy(("LP", l0, l0 + CW), pn)
+                if not last:
+                    ws = ("WS", 128 * p + cw[0], 128 * p + cw[1])
+                    tt(ws, ("PB%d" % a, 128, 128 + CW), ("M2",) + cw, ALU.subtract)
+                    j = send([ws], ("WL",) + ws[1:], prv) if p == 0 else None
+                    gact(run("XG", a), XW, ("LP", l0, l0 + CW), C_OFF * 2.0 ** p, 2.0 ** p)
+                    send([run("V", a), run("XG", a)], run("V", a, p + 1), nxt, j)
+                    continue
+                for c0 in range(0, CS, 512):
+                    s0 = a * CS + c0
+                    lp = ("LP", l0 + c0 // 16, l0 + c0 // 16 + 32)
+                    df, yq = ("DF", s0, s0 + 512), ("YQ", s0, s0 + 512)
+                    if a == NCH - 1:
+                        gtt(df, XW, lp, ("QF", c0, c0 + 512), ALU.add)
+                        ts(yq, df, 0.5, -129.0, ALU.mult, ALU.add)
+                    else:
+                        xg, ps = ("XG", p * R + s0, p * R + s0 + 512), (("PL0", "PA0")[c0 // 512], 0, 512)
+                        gact(xg, XW, lp, -0.5)
+                        mm(ps, [(MI, xg), (MI, ("QR", p * R + s0, p * R + s0 + 512))])
+                        act(df, ps, ACT.Identity, 192.0, 0.5)
+                        act(yq, df, ACT.Identity, -192.0)
+                    dma("s", T.yq[:, s0:s0 + 512], ap(yq), [yq], [], 1 << 17)
+            if p == 0 and h == 2:
+                for r, name in ((2, "SXS"), (3, "IDH"), (4, "IDL")):
+                    dma("s", T.TB[r:128:16, 0:W], T[name][:], [(name, 0, 512)], [("TBm", 0, W)], 1 << 17)
+        if last:
+            copy(("YP", 0, 128), ("A", 256 * p, 256 * p + 128))
+            dma("a", T.yp[:], T.YP[:], [("YP", 0, 128)], [], 1 << 16)
+        elif p > 0:
+            send([("WS", 128 * p, 128 * (p + 1))], ("WL", 128 * p, 128 * (p + 1)), prv)
+
+        b = 64 * p
+        fl = ("FLB", 256 * p, 256 * (p + 1))
+        gn = ("GN", 256 * p, 256 * (p + 1))
+        c_, n_, f_, t_, c2 = [("FW", b + 16 * k, b + 16 * (k + 1)) for k in range(5)]
+        gact(("GC", 0, 256), TW, ("LW", b, b + 16))
+        mm(("PN", 0, 16), wrap(Z_L1, "GC", 0, 256))
+        copy(("LW", b + 16, b + 32), ("PN", 0, 16))
+        if not last:
+            act(n_, ("PN", 0, 16))
+        mm(("PW", 16, 32), wrap(Z_ID, "FLB", 256 * p, 256))
+        act(f_, ("PW", 16, 32))
+        if p == 0:
+            act(c2, ("PW", 16, 32))
+            act(t_, c_)
+        else:
+            hp = ("H", 16 * p, 16 * (p + 1))
+            act(("F2", 0, 16), ("PW", 16, 32), ACT.Identity, 256.0)
+            ts(hp, f_, float(W), 16384.0, ALU.is_lt, ALU.mult)
+            tt(("T1", 0, 16), ("F2", 0, 16), hp, ALU.subtract)
+            tt(t_, c_, ("T1", 0, 16), ALU.max)
+            if not last:
+                tt(("C1", 0, 16), c_, hp, ALU.max)
+                tt(c2, ("C1", 0, 16), f_, ALU.min)
+        e = b + (64 if last else 80)
+        copy(("LW", b + 32, e), ("FW", b + 32, e))
+        gact(gn, TW, ("LW", b + 16, b + 32))
+        terms = [(("MPn", 0, 128), gn), (("MPf", 0, 128), fl)]
+        if not last:
+            gact(("XCN", 0, 512), XW, ("LW", b, b + 32), -0.125, 0.5)
+            mm(("PN", 128, 384), [(MI, ("XCN", 0, 256)), (MI, ("XCN", 256, 512))])
+            act(("XF", 0, 256), ("PN", 128, 384), ACT.Identity, 192.0)
+            terms.append((z(Z_S, 2), ("XF", 0, 256)))
+        mm(("PN", 256, 512), [(("MPc", 0, 128), ("GC", 0, 256)), (("MPm", 0, 128), fl)])
+        mm(("PN", 0, 256), terms)
+        act(("NCS", 0, 512), ("PN", 0, 512))
+        scatter(("TO" if last else "TB", 0, WT), ("LW", b + 32, b + 64), ("NCS", 0, 512))
+        if last:
+            dma("g", T.yn[:], T.TO[0:128:16, 0:W], [("TO", 0, W)], [("YN", 0, 1)], 1 << 18)
+            dma("g", T.yn[:], T.TO[1:128:16, 0:W], [("TO", 0, W)], [("YN", 0, 1)], 1 << 19, accum_op=ALU.add, max_dma_last_dim=4096)
+            break
+        scatter(("X", 0, WT), ("LW", b + 32, b + 48), ("XF", 0, 256), ("M192", 0, 256))
+        if p == PH - 2:
+            for r in range(2):
+                dma("s", T.TO[r:128:16, 0:W], T.TB[r:128:16, 0:W], [TW], [("TOm", 0, W)], 1 << 17)
+
+        n = 16 * (p + 1)
+        old = ("PIN", 0, 128) if p == 0 else ("A", 256 * (p - 1), 256 * (p - 1) + 128)
+        tt(("A", 256 * p + 128, 256 * (p + 1)), old, ("WL", 128 * p, 128 * (p + 1)), ALU.max)
+        for k in range(p + 1):
+            gtt(("E", 256 * k, 256 * (k + 1)), ("FW", 64 * k + 16, 64 * k + 32), ("REP", 0, 16), ("A", 256 * p, 256 * (p + 1)), ALU.is_equal)
+            terms = [(MI, ("E", 256 * k + 16 * s, 256 * k + 16 * (s + 1))) for s in range(16)] + [(MI, ("H", 16 * k, 16 * (k + 1)))]
+            terms += [(MI, ("U", 48 * m + 16 * k, 48 * m + 16 * (k + 1))) for m in range(k, p)]
+            mm(("PW", 32 + 16 * k, 48 + 16 * k), terms)
+        u = ("U", 48 * p, 48 * p + n)
+        ts(u, ("PW", 32, 32 + n), 16384.0, None, ALU.is_equal)
+        add("v", lambda q, u=u, n=n: q.tensor_tensor_scan(T.S[:, 0:n], ap(u), ap(u), 0.0, ALU.add, ALU.max), [u], [("S", 0, n)], cy(n, 1))
+        mm(("PW", 80, 80 + n), [(("MBN", 0, 128), ("S", 0, n)), (("MBN", 128, 256), u)])
+        if p < PH - 2:
+            mm(("PW", 384, 385), [(("MBN", 0, 128), ("S", n - 1, n))])
+        tt(("TM", 0, n), ("TT", 0, n), ("PW", 80, 80 + n), ALU.min)
+        bc = ("BC", 8 * p, 8 * p + 1)
+        ts(("TG", 0, n), ("TM", 0, n), bc, None, ALU.add)
+        if p < PH - 2:
+            ts(("BC", 8 * p + 8, 8 * p + 9), ("PW", 384, 385), bc, 256.0 * (p + 2) + 4095.0, ALU.add, ALU.max)
+        scatter(("FLB", 0, FLW), ("TG", 0, n), ("GN", 0, 16 * n))
+    return ops
+
+
+def depend(ops):
+    hist = {}
+    deps = []
+    for i, o in enumerate(ops):
+        d = set()
+        for r, w in [(r, False) for r in o["rd"]] + [(r, True) for r in o["wr"]]:
+            name, lo, hi = r[0], r[1], r[2]
+            part = name not in SCRATCH and name.endswith("m")
+            if part:
+                name = name[:-1]
+            psum = name in SCRATCH and SCRATCH[name][0] == "psum"
+            for (j, l2, h2, w2, p2) in hist.get(name, []):
+                if j == i:
+                    continue
+                if psum:
+                    if ops[j]["eng"] != o["eng"] or (w and l2 < hi and lo < h2):
+                        d.add(j)
+                elif (w or w2) and l2 < hi and lo < h2 and not (part and p2):
+                    d.add(j)
+            hist.setdefault(name, []).append((i, lo, hi, w, part))
+        deps.append(d)
+    reach = []
+    for i, d in enumerate(deps):
+        far = set()
+        for j in d:
+            far |= reach[j]
+        reach.append(far | d)
+        deps[i] = sorted(d - far)
+    return deps
+
+
+def timer(ops, deps, par):
+    cyc, ga, sc, pc, fix, hop, bw, dl, rl = par
+    k = {"c": cyc, "g": cyc * ga, "s": cyc * sc, "p": pc}
+    dur = [o["cost"][1] if o["cost"][0] == "n" else fix + k[o["cost"][0]] * o["cost"][1] for o in ops]
+    lat = [{"c": 0.0, "dma": dl, "send": rl, "arrive": 200.0}[o["kind"]] for o in ops]
+    bt = [o["bytes"] / bw for o in ops]
+    n = len(ops)
+    eng = ["vapgsn".index(o["eng"]) for o in ops]
+    dd = [list(deps[i]) + ([o["after"]] if o["kind"] == "arrive" else []) for i, o in enumerate(ops)]
+
+    def run(order):
+        end, start, free, bus = [0.0] * n, [0.0] * n, [0.0] * 6, 0.0
+        for i in order:
+            e = eng[i]
+            t = free[e]
+            for j in dd[i]:
+                if end[j] > t:
+                    t = end[j]
+            start[i] = t
+            t += dur[i]
+            free[e] = t
+            if bt[i]:
+                t += lat[i]
+                bus = (bus if bus > t else t) + bt[i]
+                end[i] = bus + hop
+            else:
+                end[i] = t + lat[i] + hop
+        return max(end), start
+    return run, dur, [lat[i] + bt[i] + hop for i in range(n)]
+
+
+def arrange(ops, deps):
+    n = len(ops)
+    timers = [timer(ops, deps, par) for par in GUESS]
+    runs = [t[0] for t in timers]
+    dur, lag = timers[0][1:]
+    eng = [o["eng"] for o in ops]
+    pre = [set(deps[i]) | ({o["after"]} if o["after"] is not None else set()) for i, o in enumerate(ops)]
+    post = [set() for _ in range(n)]
+    prio = [0.0] * n
+    for i in range(n - 1, -1, -1):
+        prio[i] += dur[i] + lag[i]
+        for j in pre[i]:
+            post[j].add(i)
+            queued = j not in deps[i] and ops[i]["kind"] != "arrive"
+            prio[j] = max(prio[j], prio[i] - (lag[j] if queued else 0.0))
+    prio = [prio[i] + (2000.0 if dur[i] < 400.0 else 0.0) for i in range(n)]
+    left = [len(s) for s in pre]
+    ready = [i for i in range(n) if not left[i]]
+    rt, free, cur = [0.0] * n, {e: 0.0 for e in eng}, []
+    while ready:
+        t, e = min((max(free[eng[i]], rt[i]), eng[i]) for i in ready)
+        i = max((k for k in ready if eng[k] == e and rt[k] <= t + 150.0), key=lambda k: prio[k])
+        ready.remove(i)
+        cur.append(i)
+        t = max(t, rt[i])
+        free[e] = t + dur[i]
+        for u in post[i]:
+            queued = i not in deps[u] and ops[u]["kind"] != "arrive"
+            rt[u] = max(rt[u], t if queued else free[e] + lag[i])
+            left[u] -= 1
+            if not left[u]:
+                ready.append(u)
+
+    def score(o):
+        t, s = runs[0](o)
+        return 2.0 * t + sum(s) / n + sum(r(o)[0] for r in runs[1:])
+    iters = OPT["iters"]
+    rng = np.random.RandomState(OPT["seed"])
+    pick, jump, side, luck = rng.randint(0, n, iters), rng.randint(1, 4, iters), rng.randint(0, 2, iters), rng.random_sample(iters)
+    sc = score(cur)
+    best, bs = cur, sc
+    for it in range(iters):
+        a = int(pick[it])
+        v = cur[a]
+        step, rel = (1, post) if side[it] else (-1, pre)
+        b, todo, drag, block = a, int(jump[it]), [v], set(rel[v])
+        while todo:
+            b += step
+            if b < 0 or b >= n:
+                break
+            u = cur[b]
+            if u in block:
+                if eng[u] == eng[v] or len(drag) > 3:
+                    break
+                drag.append(u)
+                block |= rel[u]
+            elif eng[u] == eng[v]:
+                todo -= 1
+        if todo:
+            continue
+        ds = set(drag)
+        if step == 1:
+            new = cur[:a] + [u for u in cur[a:b + 1] if u not in ds] + drag + cur[b + 1:]
+        else:
+            new = cur[:b] + drag[::-1] + [u for u in cur[b:a + 1] if u not in ds] + cur[a + 1:]
+        s = score(new)
+        if s <= sc or luck[it] < math.exp((sc - s) / (300.0 * (1.0 - it / iters) + 1.0)):
+            cur, sc = new, s
+            if s < bs:
+                best, bs = new, s
+    return best, [r(best)[0] for r in runs], runs[0](best)[1], dur
+
+
+ORDER = []
+
+
+def rank_program(g, core, T, topo):
+    rank = T.rank_of(core)
+    if rank is None:
+        return
+    N = len(T.cores)
+
+    def way(dst):
+        rid, pid, _ = topo.addr(dst)
+        return rid, pid, topo.mask(core, dst), len(topo.engines(core, dst))
+
+    ops = plan(T, way(T.cores[(rank + 1) % N]), way(T.cores[(rank - 1) % N]))
+    deps = depend(ops)
+    if not ORDER:
+        ORDER.extend(arrange(ops, deps)[0])
+    queue = {"v": g.vector, "a": g.scalar, "p": g.tensor, "g": g, "s": g.sync}
+    count = {}
+    mark = {}
+    clock = {}
+    known = {e: {} for e in queue}
+    for i in ORDER:
+        o = ops[i]
+        e = o["eng"]
+        s = o["sem"] or "e" + e
+        count[s] = count.get(s, 0) + o["n"]
+        mark[i] = (s, count[s])
+        if e == "n":
+            clock[i] = {s: count[s]}
+            continue
+        kn = known[e]
+        for j in sorted(deps[i], key=lambda j: -mark[j][1]):
+            if e == "p" and ops[j]["eng"] == "p":
+                continue
+            sj, cj = mark[j]
+            if kn.get(sj, 0) < cj:
+                queue[e].wait_ge(T.sem[sj], cj)
+                for k, v in clock[j].items():
+                    if kn.get(k, 0) < v:
+                        kn[k] = v
+        ins = o["fn"](queue[e])
+        if o["kind"] != "send":
+            ins.then_inc(T.sem[s], o["n"])
+        clock[i] = dict(kn)
+        clock[i][s] = count[s]
+    for s, c in count.items():
+        g.wait_ge(T.sem[s], c)

@@ -7,46 +7,51 @@ W, C, R, PH = 8192, 256, 2048, 4
 NCH = 2
 CS = R // NCH
 CW = CS // 16
-WT = W + 512
+WT = W + 256
 ZW = 144
-Z_ID, Z_K1, Z_K2, Z_K3, Z_L3, Z_L2, Z_L1, Z_A, Z_Q, Z_M, Z_S = range(11)
-NZ = 11
+Z_L, Z_V, Z_K, Z_Q, Z_M, Z_S = range(6)
+NZ = 6
 FLW = 2432
 A_OFF = [241.0, 177.0, 145.0, 129.0]
 C_OFF = 112.5
-OPT = {"neg0": {(3, 0), (3, 1)}, "pre": 1, "fill": 3, "iters": 90000, "seed": 1}
+OPT = {"neg": {(0, 2, 0), (0, 3, 0), (0, 3, 1)}, "conv": {(p, 1): "a" for p in (1, 2, 3)}, "xg": {(p, 1): "v" for p in (0, 1, 2)},
+       "hops": {(p, 1): (1, 3, 2) for p in (1, 2, 3)},
+       "gv": set(), "init": "vd", "pre": 3, "fill": 3, "seed": 1, "size": 80, "sweeps": 60, "moves": 1500, "heat": 200.0, "early": 1.0,
+       "vseq": [[("X", 0, 0), ("X", 1, 0), ("X", 2, 0), ("X", 0, 1), ("X", 1, 1), ("X", 2, 1), ("XG",), ("Xf",)],
+                [("X", 0, 0), ("E",), ("X", 1, 0), ("X", 2, 0), ("F",), ("X", 0, 1), ("X", 1, 1), ("X", 2, 1), ("XG",), ("Xf",)]]}
 
 BF, F32, I32, U16 = "bfloat16", "float32", "int32", "uint16"
 SCRATCH = {name: ("sbuf", [128, n], dtype) for name, n, dtype in (
-    ("X", WT, BF), ("TB", WT, BF), ("TO", WT, BF), ("ZB", NZ * ZW, BF),
-    ("MI", 128, BF), ("MPc", 128, BF), ("MPm", 128, BF), ("MPn", 128, BF), ("MPf", 128, BF), ("MBN", 256, BF),
-    ("NXI", 512, I32), ("NXH", 512, BF), ("NXL", 512, BF), ("IDA", 512, BF), ("IDH", 512, BF), ("IDL", 512, BF), ("SXS", 512, BF),
+    ("X", WT, BF), ("TB", WT, BF), ("TO", WT, F32), ("NC", 512, F32), ("ZB", NZ * ZW, BF),
+    ("MI", 128, BF), ("MP", 512, BF), ("MBN", 256, BF),
+    ("NXI", 512, I32), ("NXH", 512, BF), ("NXL", 512, BF), ("SXS", 512, BF), ("IDA", 512, BF), ("IDH", 512, BF), ("IDL", 512, BF), ("RD", 8, F32),
     ("FI0", 80, I32), ("FI1", 80, I32), ("FI", 80, I32), ("FH", 80, BF), ("FL", 80, BF), ("FLB", FLW, BF),
-    ("PI0", 8, I32), ("PI1", 8, I32), ("RC", 8, F32), ("RD", 8, F32), ("I16", 48, F32), ("TT", 48, F32), ("REP", 16, U16),
-    ("PIN", 128, I32), ("THI", 128, I32), ("TH", 128, BF), ("CUI", 16, I32),
-    ("LP", 128 * (PH + 1), U16), ("LN", 128 * 3, U16), ("G", 4 * R, BF), ("MN", 3 * R, BF), ("DF", 3 * R, BF),
+    ("PI0", 8, I32), ("PI1", 8, I32), ("RC", 8, F32), ("I16", 48, F32), ("TT", 48, F32), ("REP", 16, U16),
+    ("PIN", 128, I32), ("THI", 128, I32), ("TH", 128, BF), ("CH", 3 * CW, BF), ("CUI", 16, I32),
+    ("LP", 128 * (PH + 1), U16), ("LN", 128 * 3, U16), ("G", 3 * R, BF), ("MN", 3 * R, BF), ("DF", 3 * R, BF),
     ("QR", PH * R, BF), ("V", PH * R, BF), ("XG", PH * R, BF), ("QF", CS, F32), ("YQ", R, BF),
-    ("K1S", 128, F32), ("M1", 128, F32), ("M2", 128, I32), ("A", 256 * PH, I32), ("WS", 128 * 3, BF), ("WL", 128 * 3, BF),
-    ("YP", 128, F32), ("LW", 64 * PH + 16, U16), ("FW", 64 * PH + 16, F32), ("F2", 16, F32), ("C1", 16, F32), ("T1", 16, F32),
-    ("H", 16 * PH, BF), ("GC", 256, BF), ("GN", 256 * PH, BF), ("XCN", 512, BF), ("XF", 256, BF), ("M192", 256, BF),
+    ("K1S", 128, F32), ("M1", 128, F32), ("M2", 128 * PH, I32), ("A", 256 * PH, I32), ("OP", 128 * 3, I32),
+    ("YP", 128, F32), ("LW", 64 * PH + 16, U16), ("FW", 64 * PH + 16, F32), ("T1", 16, F32),
+    ("H", 16 * PH, BF), ("GC", 256 * PH, BF), ("GN", 256, BF), ("XCN", 512, BF), ("XF", 256, BF), ("M192", 256, BF),
     ("NCS", 512, BF), ("E", 768, BF), ("U", 48 * 3, BF), ("S", 48, BF), ("TM", 48, F32), ("TG", 48, U16), ("BC", 24, F32))}
 SCRATCH.update({name: ("psum", [128, 512], F32) for name in ("PL0", "PL1", "PA0", "PA1", "PB0", "PB1", "PW", "PN")})
 SEMAPHORES = (["ev", "ea", "ep", "eg"] + ["d%d" % i for i in range(40)]
-              + ["arr%d" % i for i in range(10)] + ["out%d" % i for i in range(10)])
+              + ["arr%d" % i for i in range(12)] + ["out%d" % i for i in range(12)])
 
-GUESS = [(1.0, 1.5, 3.5, 0.55, 60.0, 120.0, 200.0, 1800.0, 2000.0),
-         (1.0, 1.1, 5.0, 0.45, 50.0, 200.0, 300.0, 1500.0, 4000.0),
-         (1.1, 2.0, 2.0, 0.80, 60.0, 80.0, 150.0, 2000.0, 2000.0),
-         (1.0, 1.5, 3.8, 0.45, 60.0, 250.0, 350.0, 2200.0, 3000.0)]
+GUESS = [(1.0, 1.1, 2.6, 0.37, 60.0, 140.0, 400.0, 1600.0, 1900.0),
+         (0.85, 1.1, 2.0, 0.34, 55.0, 100.0, 450.0, 1300.0, 1500.0),
+         (1.2, 1.6, 4.5, 0.45, 60.0, 150.0, 300.0, 1800.0, 2500.0),
+         (0.9, 1.6, 4.0, 0.42, 60.0, 200.0, 250.0, 1800.0, 2500.0)]
 
 
 def plan(T, nxt, prv):
     ops = []
     cnt = {"d": 0, "r": 0}
+    tag = {}
 
     def add(eng, fn, rd, wr, cost, kind="c", sem=None, n=1, after=None, nbytes=0):
         ops.append({"eng": eng, "fn": fn, "rd": rd, "wr": wr, "cost": cost, "kind": kind, "sem": sem, "n": n,
-                    "after": after, "bytes": nbytes})
+                    "after": after, "also": set(), "bytes": nbytes})
         return len(ops) - 1
 
     def ap(r):
@@ -90,25 +95,30 @@ def plan(T, nxt, prv):
         add("v", fn, rd, [o], cy(width(o), 0.5 if two(o, i) else 1))
 
     def gtt(o, win, lst, b, op):
-        add("v", lambda q: q.tensor_tensor(ap(o), ind(win, lst), ap(b), op), [win, lst, b], [o], ("g", width(o)))
+        return add("v", lambda q: q.tensor_tensor(ap(o), ind(win, lst), ap(b), op), [win, lst, b], [o], ("g", width(o)))
 
     def scatter(win, lst, src, more=None):
         if more is None:
-            add("v", lambda q: q.tensor_copy(ind(win, lst), ap(src)), [lst, src], [win], ("s", width(src)))
-        else:
-            add("v", lambda q: q.tensor_tensor(ind(win, lst), ap(src), ap(more), ALU.add), [lst, src, more], [win], ("s", width(src)))
+            return add("v", lambda q: q.tensor_copy(ind(win, lst), ap(src)), [lst, src], [win], ("s", width(src)))
+        return add("v", lambda q: q.tensor_tensor(ind(win, lst), ap(src), ap(more), ALU.add), [lst, src, more], [win], ("s", width(src)))
 
     def act(o, i, func=ACT.Identity, bias=0.0, scale=1.0):
         return add("a", lambda q: q.activation(ap(o), ap(i), func, bias, scale), [i], [o], cy(width(o), 1))
 
-    def gact(o, win, lst, bias=0.0, scale=1.0):
-        add("a", lambda q: q.activation(ap(o), ind(win, lst), ACT.Identity, bias, scale), [win, lst], [o], ("g", width(o)))
+    def affine(eng, o, i, scale, bias):
+        if eng == "v":
+            ts(o, i, scale, bias, ALU.mult, ALU.add)
+        else:
+            act(o, i, ACT.Identity, bias, scale)
 
-    def mm(o, terms):
+    def gact(o, win, lst, bias=0.0, scale=1.0):
+        return add("a", lambda q: q.activation(ap(o), ind(win, lst), ACT.Identity, bias, scale), [win, lst], [o], ("g", width(o)))
+
+    def mm(o, terms, fresh=True, done=True):
         def fn(q):
             ins = None
             for k, (l, r) in enumerate(terms):
-                ins = q.matmul(ap(o), ap(l), ap(r), k == 0, k == len(terms) - 1)
+                ins = q.matmul(ap(o), ap(l), ap(r), fresh and k == 0, done and k == len(terms) - 1)
             return ins
         rd = []
         for l, r in terms:
@@ -131,7 +141,7 @@ def plan(T, nxt, prv):
             fn = lambda q: q.iota(ap(o), pattern, base, cm, allow_small_or_imprecise_dtypes=True)
         add("g", fn, [], [o], ("n", 160.0 + 2 * width(o)))
 
-    def send(srcs, dst, to, after=None):
+    def send(srcs, dst, to, op=1, after=None):
         k = cnt["r"]
         cnt["r"] += 1
         rid, pid, mask, ne = to
@@ -141,8 +151,9 @@ def plan(T, nxt, prv):
         else:
             fn = lambda q: q.remote_dma_fused([RemoteDMATransfer(
                 dst_ids=[DstId(rid=rid, pnc=pid)], dma_engine_mask=mask, remote_sem=T.sem[arr],
-                srcs=[ap(s) for s in srcs], dsts=[ap(dst)], alu_op=1)], local_sem=T.sem[out])
-        i = add("g", fn, list(srcs), [], ("n", 600.0 if k else 2000.0), "send", out, ne, after, 256 * width(dst) * len(srcs))
+                srcs=[ap(s) for s in srcs], dsts=[ap(dst)], alu_op=op)], local_sem=T.sem[out])
+        i = add("g", fn, list(srcs), [], ("n", 600.0 if k else 2000.0), "send", out, ne, after,
+                (256 if two(dst) else 512) * width(dst) * len(srcs))
         add("n", None, [], [dst], ("n", 0.0), "arrive", arr, ne, after=i)
         return i
 
@@ -160,60 +171,58 @@ def plan(T, nxt, prv):
     for k in range(fill):
         ops[act(("TB", 1024 * (k + 1), 1024 * (k + 2)), ("TB", 0, 1024))]["after"] = j
     memset(("TB", 1024 * (fill + 1), W), 1.0)
-    memset(("ZB", Z_L3 * ZW, Z_A * ZW), 0.0)
-    memset(("ZB", 0, Z_L3 * ZW), 0.0)
-    memset(("ZB", Z_A * ZW, NZ * ZW), 0.0)
     copy(("NXH", 0, 512), ("NXI", 0, 512))
     tt(("NXL", 0, 512), ("NXI", 0, 512), ("NXH", 0, 512), ALU.subtract)
     i = dma("s", T.TB[0:128:16, 0:W], T.NXH[:], [("NXH", 0, 512)], [("TBm", 0, W)], 1 << 17, i)
     i = dma("s", T.TB[1:128:16, 0:W], T.NXL[:], [("NXL", 0, 512)], [("TBm", 0, W)], 1 << 17, i)
+    i = dma("s", T.THI[:], T.th[:], [], [("THI", 0, 128)], 1 << 16, i)
     i = load("QR", T.q, 0, CS, i)
     for k in range(OPT["pre"], 4):
         i = load("X", T.x, 2048 * k, 2048 * (k + 1), i)
     i = load("QR", T.q, CS, R, i)
-    i = dma("s", T.THI[:], T.th[:], [], [("THI", 0, 128)], 1 << 16, i)
     copy(("LP", 0, 128), ("PIN", 0, 128))
 
-    def zrow(s0, s1, r, v):
-        return sel(("ZB", s0 * ZW + 15, s1 * ZW, 16), [[0, s1 - s0], [-16, 9]], ALU.not_equal, v, -r, 1)
-    zrow(Z_L3, Z_L1 + 1, 0, 1.0)
-    j = zrow(Z_L3, Z_L1 + 1, 1, 1.0)
-    dma("g", T.CUI[:], T.cu[:], [], [("CUI", 0, 16)], 1 << 13, j)
-    zrow(Z_L2, Z_L2 + 1, 5, 8192.0)
-    zrow(Z_K3, Z_L3 + 1, 5, 16384.0)
-    zrow(Z_K2, Z_K2 + 1, 5, 8192.0)
-    zrow(Z_ID, Z_K3 + 1, 3, 1.0)
-    zrow(Z_ID, Z_K3 + 1, 4, 1.0)
-    zrow(Z_K1, Z_K3 + 1, 2, 32768.0)
-    for s, v in ((Z_A, 32768.0), (Z_Q, -32768.0), (Z_M, -65536.0), (Z_S, 1.0)):
-        memset(("ZB", s * ZW + 15, (s + 1) * ZW, 16), v)
-    zb = ("ZB", Z_A * ZW + 15, NZ * ZW, 16)
-    sel(zb, [[0, 4], [-16, 9]], ALU.is_ge, 0.0, 0, 1)
-    sel(zb, [[0, 4], [16, 9]], ALU.is_ge, 0.0, 15, -1)
     memset(MI, 1.0)
-    sel(MI, [[-1, 128]], ALU.is_equal, 0.0, 0, 1)
+    j = sel(MI, [[-1, 128]], ALU.is_equal, 0.0, 0, 1)
+    dma("g", T.CUI[:], T.cu[:], [], [("CUI", 0, 16)], 1 << 13, j)
+    send([("PIN", 0, 128)], ("OP", 0, 128), nxt)
     memset(("MBN", 0, 128), 1.0)
     memset(("MBN", 128, 256), -1.0)
     sel(("MBN", 0, 256), [[0, 2], [-16, 8], [0, 16]], ALU.is_ge, 0.0, 0, 1)
     sel(("MBN", 0, 256), [[0, 2], [16, 8], [0, 16]], ALU.is_ge, 0.0, 15, -1)
     sel(("MBN", 128, 256), [[-1, 128]], ALU.is_ge, 0.0, 0, 1)
     sel(("MBN", 128, 256), [[-1, 128]], ALU.not_equal, -4096.0, 0, 1)
-    for name, pairs in (("MPc", ((2, 2, 1.0), (3, 3, 1.0), (4, 4, 1.0), (5, 5, 1.0))), ("MPm", ((0, 3, 1.0), (1, 4, 1.0))),
-                        ("MPn", ((0, 0, 1.0), (1, 1, 1.0), (5, 5, 1.0), (2, 5, -3072.0))), ("MPf", ((3, 3, 1.0), (4, 4, 1.0)))):
-        memset((name, 0, 128), 0.0)
-        for dst, src, v in pairs:
-            sel((name, dst, 128, 16), [[-16, 8]], ALU.not_equal, v, -src, 1)
+
+    def row(r):
+        return ("MI", r, 128, 16)
+
+    def zc(s):
+        return ("ZB", s * ZW + 15, s * ZW + 143, 16)
+    memset(("ZB", 0, NZ * ZW), 0.0)
+    tt(zc(Z_L), row(0), row(1), ALU.add)
+    ts(zc(Z_V), row(5), -16384.0, None, ALU.mult)
+    tt(zc(Z_V), zc(Z_V), zc(Z_L), ALU.add)
+    ts(zc(Z_K), row(2), -32768.0, None, ALU.mult)
+    tt(zc(Z_K), zc(Z_K), row(3), ALU.add)
+    tt(zc(Z_K), zc(Z_K), row(4), ALU.add)
+    for s, v in ((Z_Q, -32768.0), (Z_M, 65536.0), (Z_S, 1.0)):
+        ts(zc(s), ("MBN", 0, 128, 16), v, None, ALU.mult)
+    MPc, MPn, MPm, MPf = [("MP", 128 * k, 128 * (k + 1)) for k in range(4)]
+    memset(("MP", 0, 512), 0.0)
+    for m0, m1, dst, src, v in ((0, 2, 5, 5, 1.0), (1, 3, 0, 0, 1.0), (1, 3, 1, 1, 1.0), (0, 1, 3, 3, 1.0), (0, 1, 4, 4, 1.0),
+                                (0, 1, 2, 5, 4.0), (1, 2, 2, 5, -3072.0), (3, 4, 3, 0, 1.0), (3, 4, 4, 1, 1.0)):
+        sel(("MP", 128 * m0 + dst, 128 * m1, 16), [[0, m1 - m0], [-16, 8]], ALU.not_equal, v, -src, 1)
 
     iota(("PI0", 0, 1), [[0, 1]], 0, 1)
     ts(("PI1", 0, 1), ("PI0", 0, 1), 15, None, ALU.bitwise_and)
     copy(("RC", 0, 1), ("PI1", 0, 1))
     ts(("RD", 0, 1), ("PI1", 0, 1), 512.0, None, ALU.mult)
-    iota(("I16", 0, 48), [[16, 48]], 832 - 4095, 0)
-    ts(("TT", 0, 48), ("I16", 0, 48), ("RC", 0, 1), None, ALU.add)
-    ts(("REP", 0, 16), ("I16", 0, 16), 0.0, ("RC", 0, 1), ALU.mult, ALU.add)
     iota(("IDL", 0, 512), [[0, 8], [1, 64]], 0, 0)
     iota(("IDA", 0, 512), [[64, 8], [0, 64]], 0, 0)
     ts(("IDH", 0, 512), ("IDA", 0, 512), ("RD", 0, 1), None, ALU.add)
+    iota(("I16", 0, 48), [[16, 48]], 832 - 4095, 0)
+    ts(("TT", 0, 48), ("I16", 0, 48), ("RC", 0, 1), None, ALU.add)
+    ts(("REP", 0, 16), ("I16", 0, 16), 0.0, ("RC", 0, 1), ALU.mult, ALU.add)
     iota(("FI0", 0, 80), [[1, 80]], 0, 80)
     ts(("FI1", 0, 80), ("FI0", 0, 80), 255, None, ALU.bitwise_and)
     ts(("FI", 0, 80), ("FI1", 0, 80), float(W), None, ALU.add)
@@ -221,19 +230,26 @@ def plan(T, nxt, prv):
         dma("s", T.FI[k:128:16, 0:80], T.fr[:, 80 * k:80 * (k + 1)], [], [("FIm", 0, 80)], 2560, i)
     copy(("FH", 0, 80), ("FI", 0, 80))
     tt(("FL", 0, 80), ("FI", 0, 80), ("FH", 0, 80), ALU.subtract)
-    memset(("FLB", 0, 1024), 0.0)
-    dma("s", T.FLB[3:128:16, 0:1280], T.FH[:], [("FH", 0, 80)], [("FLBm", 0, FLW)], 20480)
-    dma("s", T.FLB[4:128:16, 0:1280], T.FL[:], [("FL", 0, 80)], [("FLBm", 0, FLW)], 20480)
+    memset(("FLB", 0, 320), 1.0)
+    memset(("FLB", 320, 1024), 0.0)
+    dma("s", T.FLB[0:128:16, 0:1280], T.FH[:], [("FH", 0, 80)], [("FLBm", 0, FLW)], 20480)
+    dma("s", T.FLB[1:128:16, 0:1280], T.FL[:], [("FL", 0, 80)], [("FLBm", 0, FLW)], 20480)
     ts(("TH", 0, 128), ("THI", 0, 128), 32768.0, None, ALU.mult)
+    iota(("CH", 0, 3 * CW), [[-8192, 3], [0, CW]], -8192, 0)
     copy(("LW", 0, 16), ("CUI", 0, 16))
-    copy(("FW", 0, 16), ("CUI", 0, 16))
-    memset(("H", 0, 16), 16384.0)
+    memset(("H", 0, 16), -1.0)
     memset(("M192", 0, 256), -192.0)
     memset(("BC", 0, 1), 64.0 + 256.0 + 4095.0)
     for a in range(NCH):
-        ts(("V", a * CS, (a + 1) * CS), ("QR", a * CS, (a + 1) * CS), A_OFF[0], None, ALU.add)
-    mm(("PN", 0, 512), [(z(Z_S, k), ("X", 512 * k, 512 * (k + 1))) for k in range(16)])
-    act(("SXS", 0, 512), ("PN", 0, 512))
+        va = ("V", a * CS, (a + 1) * CS)
+        if OPT["init"][a] == "d":
+            memset(va, A_OFF[0])
+            dma("g", ap(va), T.q[:, a * CS:(a + 1) * CS], [va, ("X", W - 8, W)], [va], 512 * CS, accum_op=ALU.add)
+        else:
+            affine(OPT["init"][a], va, ("QR", a * CS, (a + 1) * CS), 1.0, A_OFF[0])
+    for k in range(0, 16, 4):
+        mm(("PW", 0, 512), [(z(Z_S, m), ("X", 512 * m, 512 * (m + 1))) for m in range(k, k + 4)], k == 0, k == 12)
+    act(("SXS", 0, 512), ("PW", 0, 512))
 
     for p in range(PH):
         last = p == PH - 1
@@ -244,140 +260,151 @@ def plan(T, nxt, prv):
         def run(name, a, k=p):
             return (name, k * R + a * CS, k * R + (a + 1) * CS)
 
+        def fixed(h, a):
+            return [(MI, ("CH", CW * (h - 1), CW * h))] + ([] if last else [(MI, ("TH", CW * a, CW * (a + 1)))])
+
         if p > 0:
             for a in range(NCH):
-                ts(run("QR", a), run("V", a), 0.5 ** p, -A_OFF[p], ALU.mult, ALU.add)
+                affine(OPT["conv"].get((p, a), "v"), run("QR", a), run("V", a), 0.5 ** p, -A_OFF[p])
         if last:
             act(("QF", 0, CS), run("QR", NCH - 1), ACT.Identity, 257.5)
-        for h in range(4):
+        for h in range(3):
             for a in range(NCH):
-                if h < 3 or p > 0:
-                    gact(run("G", a, h), TW, lst(h, a))
-                if h < 3:
-                    mm(("PL%d" % a, 0, CW), wrap(Z_L1, "G", h * R + a * CS, CS))
-                    copy(lst(h + 1, a), ("PL%d" % a, 0, CW))
-            for a in range(NCH):
-                if h == 0:
-                    if not last:
-                        terms = [(MI, ("TH", CW * a, CW * (a + 1)))]
-                        if p > 0:
-                            terms += wrap(Z_Q, "QR", p * R + a * CS, CS)
-                        mm(("PB%d" % a, 128, 128 + CW), terms)
-                    continue
+                if (p, h, a) in OPT["gv"]:
+                    add("v", lambda q, o=run("G", a, h), l=lst(h, a): q.tensor_copy(ap(o), ind(TW, l)),
+                        [TW, lst(h, a)], [run("G", a, h)], ("g", CS))
+                else:
+                    tag["G", p, h, a] = gact(run("G", a, h), TW, lst(h, a))
+                mm(("PL%d" % a, 0, CW), wrap(Z_L, "G", h * R + a * CS, CS))
+                copy(lst(h + 1, a), ("PL%d" % a, 0, CW))
+        for a in range(NCH):
+            hops = OPT["hops"].get((p, a), (1, 2, 3))
+
+            def key(h, a):
+                return (("PA%d", "PB%d", "PA%d")[hops.index(h)] % a, 0, CW)
+            for h in hops:
                 m0 = (h - 1) * R + a * CS
                 mn, df = run("MN", a, h - 1), run("DF", a, h - 1)
-                if p == 0:
-                    gtt(df, XW, lst(h, a), run("QR", a), ALU.subtract)
-                    terms = wrap((Z_L1, Z_L2, Z_L3)[h - 1], "G", m0, CS)
-                    if (h, a) in OPT["neg0"]:
+                if p == 0 or h == 3:
+                    tag["X", p, h, a] = gtt(df, XW, lst(h, a), run("QR", a), ALU.subtract)
+                    mm(key(h, a), fixed(h, a) + wrap(Z_L, "G", m0, CS), True, False)
+                    if (p, h, a) in OPT["neg"]:
                         ts(mn, df, 0.0, None, ALU.min)
-                        terms += wrap(Z_A, "DF", m0, CS) + wrap(Z_M, "MN", m0, CS)
+                        mm(key(h, a), wrap(Z_Q, "DF", m0, CS), False, False)
+                        mm(key(h, a), wrap(Z_M, "MN", m0, CS), False)
                     else:
                         act(mn, df, ACT.Abs)
-                        terms += wrap(Z_A, "MN", m0, CS)
+                        mm(key(h, a), wrap(Z_Q, "MN", m0, CS), False)
                 else:
-                    gtt(mn, XW, lst(h, a), run("QR", a), ALU.min)
-                    terms = wrap((Z_K1, Z_K2, Z_K3)[h - 1], "G", h * R + a * CS, CS) + wrap(Z_M, "MN", m0, CS)
+                    tag["X", p, h, a] = gtt(mn, XW, lst(h, a), run("QR", a), ALU.min)
+                    parts = [wrap(Z_K, "G", h * R + a * CS, CS), wrap(Z_Q, "QR", p * R + a * CS, CS)]
+                    if h == 2:
+                        parts.reverse()
+                    mm(key(h, a), fixed(h, a) + parts[0], True, False)
+                    mm(key(h, a), parts[1], False, False)
+                    mm(key(h, a), wrap(Z_M, "MN", m0, CS), False)
                 cw = (CW * a, CW * (a + 1))
-                if h == 1:
-                    mm(("PA%d" % a, 0, CW), terms)
-                    act(("K1S",) + cw, ("PA%d" % a, 0, CW))
-                    continue
-                if h == 2:
-                    mm(("PA%d" % a, 128, 128 + CW), terms)
-                    tt(("M1",) + cw, ("K1S",) + cw, ("PA%d" % a, 128, 128 + CW), ALU.min)
-                    continue
-                mm(("PB%d" % a, 0, CW), terms)
-                tt(("M2",) + cw, ("M1",) + cw, ("PB%d" % a, 0, CW), ALU.min)
-                pn = ("A", 256 * p + cw[0], 256 * p + cw[1])
-                ts(pn, ("M2",) + cw, W - 1, None, ALU.bitwise_and)
-                l0 = 128 * (p + 1) + cw[0]
-                copy(("LP", l0, l0 + CW), pn)
-                if not last:
-                    ws = ("WS", 128 * p + cw[0], 128 * p + cw[1])
-                    tt(ws, ("PB%d" % a, 128, 128 + CW), ("M2",) + cw, ALU.subtract)
-                    j = send([ws], ("WL",) + ws[1:], prv) if p == 0 else None
-                    gact(run("XG", a), XW, ("LP", l0, l0 + CW), C_OFF * 2.0 ** p, 2.0 ** p)
-                    send([run("V", a), run("XG", a)], run("V", a, p + 1), nxt, j)
-                    continue
-                for c0 in range(0, CS, 512):
-                    s0 = a * CS + c0
-                    lp = ("LP", l0 + c0 // 16, l0 + c0 // 16 + 32)
-                    df, yq = ("DF", s0, s0 + 512), ("YQ", s0, s0 + 512)
-                    if a == NCH - 1:
-                        gtt(df, XW, lp, ("QF", c0, c0 + 512), ALU.add)
-                        ts(yq, df, 0.5, -129.0, ALU.mult, ALU.add)
-                    else:
-                        xg, ps = ("XG", p * R + s0, p * R + s0 + 512), (("PL0", "PA0")[c0 // 512], 0, 512)
-                        gact(xg, XW, lp, -0.5)
-                        mm(ps, [(MI, xg), (MI, ("QR", p * R + s0, p * R + s0 + 512))])
-                        act(df, ps, ACT.Identity, 192.0, 0.5)
-                        act(yq, df, ACT.Identity, -192.0)
-                    dma("s", T.yq[:, s0:s0 + 512], ap(yq), [yq], [], 1 << 17)
-            if p == 0 and h == 2:
-                for r, name in ((2, "SXS"), (3, "IDH"), (4, "IDL")):
-                    dma("s", T.TB[r:128:16, 0:W], T[name][:], [(name, 0, 512)], [("TBm", 0, W)], 1 << 17)
+                if h == hops[0]:
+                    act(("K1S",) + cw, key(h, a))
+                elif h == hops[1]:
+                    tt(("M1",) + cw, ("K1S",) + cw, key(h, a), ALU.max)
+            m2 = ("M2", 128 * p + cw[0], 128 * p + cw[1])
+            tt(m2, ("M1",) + cw, key(hops[2], a), ALU.max)
+            pn = ("A", 256 * p + cw[0], 256 * p + cw[1])
+            ts(pn, m2, W - 1, None, ALU.bitwise_and)
+            l0 = 128 * (p + 1) + cw[0]
+            copy(("LP", l0, l0 + CW), pn)
+            if not last:
+                xg, lp = run("XG", a), ("LP", l0, l0 + CW)
+                if OPT["xg"].get((p, a), "a") == "a":
+                    tag["XG", p, a] = gact(xg, XW, lp, C_OFF * 2.0 ** p, 2.0 ** p)
+                else:
+                    tag["XG", p, a] = add("v", lambda q, xg=xg, lp=lp, s=2.0 ** p: q.tensor_scalar(
+                        ap(xg), ind(XW, lp), C_OFF, s, ALU.add, ALU.mult), [XW, lp], [xg], ("g", CS))
+                send([run("V", a), xg], run("V", a, p + 1), nxt)
+                continue
+            for c0 in range(0, CS, 512):
+                s0 = a * CS + c0
+                lp = ("LP", l0 + c0 // 16, l0 + c0 // 16 + 32)
+                df, yq = ("DF", s0, s0 + 512), ("YQ", s0, s0 + 512)
+                if a == NCH - 1:
+                    tag["Y", p, c0] = gtt(df, XW, lp, ("QF", c0, c0 + 512), ALU.add)
+                    ts(yq, df, 0.5, -129.0, ALU.mult, ALU.add)
+                else:
+                    xg, ps = ("XG", p * R + s0, p * R + s0 + 512), (("PL0", "PB0")[c0 // 512], 0, 512)
+                    gact(xg, XW, lp, -0.5)
+                    mm(ps, [(MI, xg), (MI, ("QR", p * R + s0, p * R + s0 + 512))])
+                    act(df, ps, ACT.Identity, 192.0, 0.5)
+                    act(yq, df, ACT.Identity, -192.0)
+                dma("s", T.yq[:, s0:s0 + 512], ap(yq), [yq], [], 1 << 17)
         if last:
             copy(("YP", 0, 128), ("A", 256 * p, 256 * p + 128))
             dma("a", T.yp[:], T.YP[:], [("YP", 0, 128)], [], 1 << 16)
-        elif p > 0:
-            send([("WS", 128 * p, 128 * (p + 1))], ("WL", 128 * p, 128 * (p + 1)), prv)
+        else:
+            send([("M2", 128 * p, 128 * (p + 1)), ("OP", 128 * p, 128 * (p + 1))], ("A", 256 * p + 128, 256 * (p + 1)), prv, 2)
+            if p < PH - 2:
+                send([("A", 256 * p, 256 * p + 128)], ("OP", 128 * (p + 1), 128 * (p + 2)), nxt)
 
         b = 64 * p
         fl = ("FLB", 256 * p, 256 * (p + 1))
-        gn = ("GN", 256 * p, 256 * (p + 1))
-        c_, n_, f_, t_, c2 = [("FW", b + 16 * k, b + 16 * (k + 1)) for k in range(5)]
-        gact(("GC", 0, 256), TW, ("LW", b, b + 16))
-        mm(("PN", 0, 16), wrap(Z_L1, "GC", 0, 256))
+        gc, gn = ("GC", 256 * p, 256 * (p + 1)), ("GN", 0, 256)
+        c_, n_, t_, f_, c2 = [("FW", b + 16 * k, b + 16 * (k + 1)) for k in range(5)]
+        lt, lf = ("LW", b + 32, b + 48), ("LW", b + 48, b + 64)
+        if p == 0:
+            for r, name in ((3, "IDH"), (4, "IDL")):
+                dma("s", T.TB[r:128:16, 0:W], T[name][:], [(name, 0, 512)], [("TBm", 0, W)], 1 << 17, i)
+        gact(gc, TW, ("LW", b, b + 16))
+        mm(("PN", 0, 16), wrap(Z_L, "GC", 256 * p, 256))
         copy(("LW", b + 16, b + 32), ("PN", 0, 16))
         if not last:
             act(n_, ("PN", 0, 16))
-        mm(("PW", 16, 32), wrap(Z_ID, "FLB", 256 * p, 256))
-        act(f_, ("PW", 16, 32))
+        mm(("PW", 16, 32), wrap(Z_L, "FLB", 256 * p, 256))
         if p == 0:
+            lt, lf = ("LW", 0, 16), ("LW", 64, 80)
+            copy(lf, ("PW", 16, 32))
             act(c2, ("PW", 16, 32))
-            act(t_, c_)
         else:
-            hp = ("H", 16 * p, 16 * (p + 1))
-            act(("F2", 0, 16), ("PW", 16, 32), ACT.Identity, 256.0)
-            ts(hp, f_, float(W), 16384.0, ALU.is_lt, ALU.mult)
-            tt(("T1", 0, 16), ("F2", 0, 16), hp, ALU.subtract)
-            tt(t_, c_, ("T1", 0, 16), ALU.max)
+            mm(("PW", 0, 16), wrap(Z_V, "FLB", 256 * p, 256))
+            act(f_, ("PW", 16, 32))
+            tt(t_, c_, ("PW", 0, 16), ALU.max)
             if not last:
-                tt(("C1", 0, 16), c_, hp, ALU.max)
-                tt(c2, ("C1", 0, 16), f_, ALU.min)
-        e = b + (64 if last else 80)
-        copy(("LW", b + 32, e), ("FW", b + 32, e))
+                act(("H", 16 * p, 16 * (p + 1)), ("PW", 0, 16), ACT.Sign)
+                tt(("T1", 0, 16), c_, t_, ALU.subtract)
+                tt(c2, ("T1", 0, 16), ("PW", 16, 32), ALU.add)
+            e = b + (64 if last else 80)
+            copy(("LW", b + 32, e), ("FW", b + 32, e))
         gact(gn, TW, ("LW", b + 16, b + 32))
-        terms = [(("MPn", 0, 128), gn), (("MPf", 0, 128), fl)]
-        if not last:
-            gact(("XCN", 0, 512), XW, ("LW", b, b + 32), -0.125, 0.5)
-            mm(("PN", 128, 384), [(MI, ("XCN", 0, 256)), (MI, ("XCN", 256, 512))])
-            act(("XF", 0, 256), ("PN", 128, 384), ACT.Identity, 192.0)
-            terms.append((z(Z_S, 2), ("XF", 0, 256)))
-        mm(("PN", 256, 512), [(("MPc", 0, 128), ("GC", 0, 256)), (("MPm", 0, 128), fl)])
-        mm(("PN", 0, 256), terms)
-        act(("NCS", 0, 512), ("PN", 0, 512))
-        scatter(("TO" if last else "TB", 0, WT), ("LW", b + 32, b + 64), ("NCS", 0, 512))
+        if p == 0:
+            dma("s", T.TB[2:128:16, 0:W], T.SXS[:], [("SXS", 0, 512)], [("TBm", 0, W)], 1 << 17)
         if last:
-            dma("g", T.yn[:], T.TO[0:128:16, 0:W], [("TO", 0, W)], [("YN", 0, 1)], 1 << 18)
-            dma("g", T.yn[:], T.TO[1:128:16, 0:W], [("TO", 0, W)], [("YN", 0, 1)], 1 << 19, accum_op=ALU.add, max_dma_last_dim=4096)
+            mm(("PN", 256, 512), [(z(Z_L, 0), fl)])
+            mm(("PN", 0, 256), [(z(Z_L, 0), gn)])
+            act(("NC", 0, 512), ("PN", 0, 512))
+            tag["Tc", p] = scatter(("TO", 0, WT), lt, ("NC", 256, 512))
+            tag["Tf", p] = scatter(("TO", 0, WT), lf, ("NC", 0, 256))
+            dma("s", T.yn[:], T.TO[0:128:16, 0:W], [("TO", 0, W)], [("YN", 0, 1)], 1 << 18)
             break
-        scatter(("X", 0, WT), ("LW", b + 32, b + 48), ("XF", 0, 256), ("M192", 0, 256))
+        gact(("XCN", 0, 512), XW, ("LW", b, b + 32), -0.125, 0.5)
+        mm(("PN", 256, 512), [(MI, ("XCN", 0, 256)), (MI, ("XCN", 256, 512))])
+        act(("XF", 0, 256), ("PN", 256, 512), ACT.Identity, 192.0)
+        mm(("PN", 256, 512), [(MPc, gc), (MPm, fl)] + 2 * [(z(Z_S, 2), ("XCN", 0, 256))])
+        mm(("PN", 0, 256), [(MPn, gn), (MPf, fl), (z(Z_S, 2), ("XF", 0, 256))])
+        act(("NCS", 0, 512), ("PN", 0, 512))
+        tag["Tc", p] = scatter(("TB", 0, WT), lt, ("NCS", 256, 512))
+        tag["Tf", p] = scatter(("TB", 0, WT), lf, ("NCS", 0, 256))
+        tag["Xf", p] = scatter(("X", 0, WT), lf, ("XF", 0, 256), ("M192", 0, 256))
         if p == PH - 2:
-            for r in range(2):
-                dma("s", T.TO[r:128:16, 0:W], T.TB[r:128:16, 0:W], [TW], [("TOm", 0, W)], 1 << 17)
+            dma("g", T.TO[0:128:16, 0:W], T.TB[0:128:16, 0:W], [TW], [("TO", 0, W)], 1 << 18)
+            dma("g", T.TO[0:128:16, 0:W], T.TB[1:128:16, 0:W], [TW], [("TO", 0, W)], 1 << 19, accum_op=ALU.add, max_dma_last_dim=4096)
 
         n = 16 * (p + 1)
-        old = ("PIN", 0, 128) if p == 0 else ("A", 256 * (p - 1), 256 * (p - 1) + 128)
-        tt(("A", 256 * p + 128, 256 * (p + 1)), old, ("WL", 128 * p, 128 * (p + 1)), ALU.max)
         for k in range(p + 1):
-            gtt(("E", 256 * k, 256 * (k + 1)), ("FW", 64 * k + 16, 64 * k + 32), ("REP", 0, 16), ("A", 256 * p, 256 * (p + 1)), ALU.is_equal)
+            tag["E", p, k] = gtt(("E", 256 * k, 256 * (k + 1)), ("FW", 64 * k + 16, 64 * k + 32), ("REP", 0, 16), ("A", 256 * p, 256 * (p + 1)), ALU.is_equal)
             terms = [(MI, ("E", 256 * k + 16 * s, 256 * k + 16 * (s + 1))) for s in range(16)] + [(MI, ("H", 16 * k, 16 * (k + 1)))]
             terms += [(MI, ("U", 48 * m + 16 * k, 48 * m + 16 * (k + 1))) for m in range(k, p)]
             mm(("PW", 32 + 16 * k, 48 + 16 * k), terms)
         u = ("U", 48 * p, 48 * p + n)
-        ts(u, ("PW", 32, 32 + n), 16384.0, None, ALU.is_equal)
+        act(u, ("PW", 32, 32 + n), ACT.Relu, 0.0, -1.0)
         add("v", lambda q, u=u, n=n: q.tensor_tensor_scan(T.S[:, 0:n], ap(u), ap(u), 0.0, ALU.add, ALU.max), [u], [("S", 0, n)], cy(n, 1))
         mm(("PW", 80, 80 + n), [(("MBN", 0, 128), ("S", 0, n)), (("MBN", 128, 256), u)])
         if p < PH - 2:
@@ -387,8 +414,29 @@ def plan(T, nxt, prv):
         ts(("TG", 0, n), ("TM", 0, n), bc, None, ALU.add)
         if p < PH - 2:
             ts(("BC", 8 * p + 8, 8 * p + 9), ("PW", 384, 385), bc, 256.0 * (p + 2) + 4095.0, ALU.add, ALU.max)
-        scatter(("FLB", 0, FLW), ("TG", 0, n), ("GN", 0, 16 * n))
+        tag["F", p] = scatter(("FLB", 0, FLW), ("TG", 0, n), ("GC", 0, 16 * n))
+    for chain in chains():
+        chain = [tag[t] for t in chain if t in tag]
+        for u0, u1 in zip(chain, chain[1:]):
+            ops[u1]["also"].add(u0)
     return ops
+
+
+def chains():
+    seq = []
+    for p in range(PH):
+        for t in OPT["vseq"][min(p, 1)]:
+            if t[0] == "X":
+                seq.append(("X", p, OPT["hops"].get((p, t[2]), (1, 2, 3))[t[1]], t[2]))
+            elif t[0] == "E":
+                seq += [("E", p - 1, k) for k in range(p)]
+            elif t[0] == "XG":
+                seq.append(("XG", p, 1))
+            elif t[0] == "F":
+                seq.append(("F", p - 1))
+            else:
+                seq.append((t[0], p))
+    return [seq, [("G", 0, 0, 0), ("G", 0, 0, 1)], [("Tc", PH - 1), ("Tf", PH - 1), ("Y", PH - 1, 0)]]
 
 
 def depend(ops):
@@ -432,37 +480,77 @@ def timer(ops, deps, par):
     eng = ["vapgsn".index(o["eng"]) for o in ops]
     dd = [list(deps[i]) + ([o["after"]] if o["kind"] == "arrive" else []) for i, o in enumerate(ops)]
 
-    def run(order):
-        end, start, free, bus = [0.0] * n, [0.0] * n, [0.0] * 6, 0.0
+    row = [(eng[i], dd[i], dur[i], bt[i], lat[i] + (0.0 if bt[i] else hop)) for i in range(n)]
+
+    def walk(order, end, free, tail):
+        far, both, bus = 0.0, 0.0, free[6]
         for i in order:
-            e = eng[i]
+            e, d, u, b, l = row[i]
             t = free[e]
-            for j in dd[i]:
+            for j in d:
                 if end[j] > t:
                     t = end[j]
-            start[i] = t
-            t += dur[i]
+            both += t
+            t += u
             free[e] = t
-            if bt[i]:
-                t += lat[i]
-                bus = (bus if bus > t else t) + bt[i]
-                end[i] = bus + hop
-            else:
-                end[i] = t + lat[i] + hop
-        return max(end), start
-    return run, dur, [lat[i] + bt[i] + hop for i in range(n)]
+            t += l
+            if b:
+                bus = (bus if bus > t else t) + b
+                t = bus + hop
+            end[i] = t
+            t += tail[i]
+            if t > far:
+                far = t
+        free[6] = bus
+        return far, both
+
+    def run(order):
+        end = [0.0] * n
+        far = walk(order, end, [0.0] * 7, [0.0] * n)[0]
+        start, free = [0.0] * n, [0.0] * 6
+        for i in order:
+            start[i] = max([free[eng[i]]] + [end[j] for j in dd[i]])
+            free[eng[i]] = start[i] + dur[i]
+        return far, start
+
+    def part(order, lo, hi):
+        tail, rest = [0.0] * n, [0.0] * 7
+        for i in reversed(order[hi:]):
+            e, d, u, b, l = row[i]
+            t = tail[i]
+            if b:
+                t = rest[6] = b + max(t + hop, rest[6])
+            t = rest[e] = u + max(l + t, rest[e])
+            for j in d:
+                if t > tail[j]:
+                    tail[j] = t
+        end, free0 = [0.0] * n, [0.0] * 7
+        base = walk(order[:lo], end, free0, tail)[0]
+
+        def time(stretch):
+            free = free0[:]
+            far, both = walk(stretch, end, free, tail)
+            return max(base, far, max([free[e] + rest[e] for e in range(7)])), both
+        return time
+    return run, dur, [lat[i] + bt[i] + hop for i in range(n)], part
 
 
 def arrange(ops, deps):
     n = len(ops)
     timers = [timer(ops, deps, par) for par in GUESS]
     runs = [t[0] for t in timers]
-    dur, lag = timers[0][1:]
+    dur, lag = timers[0][1:3]
     eng = [o["eng"] for o in ops]
-    pre = [set(deps[i]) | ({o["after"]} if o["after"] is not None else set()) for i, o in enumerate(ops)]
+    pre = [set(deps[i]) | o["also"] | ({o["after"]} if o["after"] is not None else set()) for i, o in enumerate(ops)]
     post = [set() for _ in range(n)]
     prio = [0.0] * n
-    for i in range(n - 1, -1, -1):
+    line, seen = [], set()
+    while len(line) < n:
+        for i in range(n):
+            if i not in seen and pre[i] <= seen:
+                seen.add(i)
+                line.append(i)
+    for i in reversed(line):
         prio[i] += dur[i] + lag[i]
         for j in pre[i]:
             post[j].add(i)
@@ -486,43 +574,54 @@ def arrange(ops, deps):
             if not left[u]:
                 ready.append(u)
 
-    def score(o):
-        t, s = runs[0](o)
-        return 2.0 * t + sum(s) / n + sum(r(o)[0] for r in runs[1:])
-    iters = OPT["iters"]
     rng = np.random.RandomState(OPT["seed"])
-    pick, jump, side, luck = rng.randint(0, n, iters), rng.randint(1, 4, iters), rng.randint(0, 2, iters), rng.random_sample(iters)
-    sc = score(cur)
-    best, bs = cur, sc
-    for it in range(iters):
-        a = int(pick[it])
-        v = cur[a]
-        step, rel = (1, post) if side[it] else (-1, pre)
-        b, todo, drag, block = a, int(jump[it]), [v], set(rel[v])
-        while todo:
-            b += step
-            if b < 0 or b >= n:
-                break
-            u = cur[b]
-            if u in block:
-                if eng[u] == eng[v] or len(drag) > 3:
-                    break
-                drag.append(u)
-                block |= rel[u]
-            elif eng[u] == eng[v]:
-                todo -= 1
-        if todo:
-            continue
-        ds = set(drag)
-        if step == 1:
-            new = cur[:a] + [u for u in cur[a:b + 1] if u not in ds] + drag + cur[b + 1:]
-        else:
-            new = cur[:b] + drag[::-1] + [u for u in cur[b:a + 1] if u not in ds] + cur[a + 1:]
-        s = score(new)
-        if s <= sc or luck[it] < math.exp((sc - s) / (300.0 * (1.0 - it / iters) + 1.0)):
-            cur, sc = new, s
-            if s < bs:
-                best, bs = new, s
+    size, sweeps, moves = OPT["size"], OPT["sweeps"], OPT["moves"]
+    best, bs = cur, 1e18
+    for sweep in range(sweeps):
+        heat = OPT["heat"] * (1.0 - sweep / sweeps) ** 2
+        for lo in range(-int(rng.randint(0, size // 2)), n - size // 2, size // 2):
+            start = runs[0](cur)[1]
+            cur = sorted(cur, key=lambda k: start[k])
+            lo, hi = max(lo, 0), min(lo + size, n)
+            times = [t[3](cur, lo, hi) for t in timers]
+
+            def score(o):
+                t, both = times[0](o)
+                return 2.0 * t + OPT["early"] * both / n + sum(f(o)[0] for f in times[1:])
+            w, m = cur[lo:hi], hi - lo
+            sc = score(w)
+            pick, jump, side, luck = [x.tolist() for x in (rng.randint(0, m, moves), rng.geometric(0.45, moves),
+                                                           rng.randint(0, 2, moves), rng.random_sample(moves))]
+            for a, todo, up, lk in zip(pick, jump, side, luck):
+                v = w[a]
+                step, rel = (1, post) if up else (-1, pre)
+                b, drag, block = a, [v], set(rel[v])
+                while todo:
+                    b += step
+                    if b < 0 or b >= m:
+                        break
+                    u = w[b]
+                    if u in block:
+                        if eng[u] == eng[v] or len(drag) > 5:
+                            break
+                        drag.append(u)
+                        block |= rel[u]
+                    elif eng[u] == eng[v]:
+                        todo -= 1
+                if todo:
+                    continue
+                ds = set(drag)
+                if step == 1:
+                    new = w[:a] + [u for u in w[a:b + 1] if u not in ds] + drag + w[b + 1:]
+                else:
+                    new = w[:b] + drag[::-1] + [u for u in w[b:a + 1] if u not in ds] + w[a + 1:]
+                s = score(new)
+                if s <= sc or lk < math.exp((sc - s) / heat):
+                    w, sc = new, s
+            cur = cur[:lo] + w + cur[hi:]
+        s = runs[0](cur)[0] + sum(r(cur)[0] for r in runs)
+        if s < bs:
+            best, bs = cur, s
     return best, [r(best)[0] for r in runs], runs[0](best)[1], dur
 
 

import math
import numpy as np
from concourse.bass import DstId, RemoteDMATransfer
from concourse.mybir import AluOpType as ALU, ActivationFunctionType as ACT

W, C, R, PH = 8192, 256, 2048, 4
NCH = 2
CS = R // NCH
CW = CS // 16
WT = W + 256
ZW = 144
Z_L, Z_V, Z_K, Z_Q, Z_M, Z_S = range(6)
NZ = 6
FLW = 2432
A_OFF = [241.0, 177.0, 145.0, 129.0]
C_OFF = 112.5
OPT = {"neg": {(0, 2, 0), (0, 3, 0), (0, 3, 1)}, "conv": {(p, 1): "a" for p in (1, 2, 3)}, "xg": {(p, 1): "v" for p in (0, 1, 2)},
       "hops": {(p, 1): (1, 3, 2) for p in (1, 2, 3)},
       "gv": set(), "init": "vd", "pre": 3, "fill": 3, "seed": 1, "size": 80, "sweeps": 60, "moves": 1500, "heat": 200.0, "early": 1.0,
       "vseq": [[("X", 0, 0), ("X", 1, 0), ("X", 2, 0), ("X", 0, 1), ("X", 1, 1), ("X", 2, 1), ("XG",), ("Xf",)],
                [("X", 0, 0), ("E",), ("X", 1, 0), ("X", 2, 0), ("F",), ("X", 0, 1), ("X", 1, 1), ("X", 2, 1), ("XG",), ("Xf",)]]}

BF, F32, I32, U16 = "bfloat16", "float32", "int32", "uint16"
SCRATCH = {name: ("sbuf", [128, n], dtype) for name, n, dtype in (
    ("X", WT, BF), ("TB", WT, BF), ("TO", WT, F32), ("NC", 512, F32), ("ZB", NZ * ZW, BF),
    ("MI", 128, BF), ("MP", 512, BF), ("MBN", 256, BF),
    ("NXI", 512, I32), ("NXH", 512, BF), ("NXL", 512, BF), ("SXS", 512, BF), ("IDA", 512, BF), ("IDH", 512, BF), ("IDL", 512, BF), ("RD", 8, F32),
    ("FI0", 80, I32), ("FI1", 80, I32), ("FI", 80, I32), ("FH", 80, BF), ("FL", 80, BF), ("FLB", FLW, BF),
    ("PI0", 8, I32), ("PI1", 8, I32), ("RC", 8, F32), ("I16", 48, F32), ("TT", 48, F32), ("REP", 16, U16),
    ("PIN", 128, I32), ("THI", 128, I32), ("TH", 128, BF), ("CH", 3 * CW, BF), ("CUI", 16, I32),
    ("LP", 128 * (PH + 1), U16), ("LN", 128 * 3, U16), ("G", 3 * R, BF), ("MN", 3 * R, BF), ("DF", 3 * R, BF),
    ("QR", PH * R, BF), ("V", PH * R, BF), ("XG", PH * R, BF), ("QF", CS, F32), ("YQ", R, BF),
    ("K1S", 128, F32), ("M1", 128, F32), ("M2", 128 * PH, I32), ("A", 256 * PH, I32), ("OP", 128 * 3, I32),
    ("YP", 128, F32), ("LW", 64 * PH + 16, U16), ("FW", 64 * PH + 16, F32), ("T1", 16, F32),
    ("H", 16 * PH, BF), ("GC", 256 * PH, BF), ("GN", 256, BF), ("XCN", 512, BF), ("XF", 256, BF), ("M192", 256, BF),
    ("NCS", 512, BF), ("E", 768, BF), ("U", 48 * 3, BF), ("S", 48, BF), ("TM", 48, F32), ("TG", 48, U16), ("BC", 24, F32))}
SCRATCH.update({name: ("psum", [128, 512], F32) for name in ("PL0", "PL1", "PA0", "PA1", "PB0", "PB1", "PW", "PN")})
SEMAPHORES = (["ev", "ea", "ep", "eg"] + ["d%d" % i for i in range(40)]
              + ["arr%d" % i for i in range(12)] + ["out%d" % i for i in range(12)])

GUESS = [(1.0, 1.1, 2.6, 0.37, 60.0, 140.0, 400.0, 1600.0, 1900.0),
         (0.85, 1.1, 2.0, 0.34, 55.0, 100.0, 450.0, 1300.0, 1500.0),
         (1.2, 1.6, 4.5, 0.45, 60.0, 150.0, 300.0, 1800.0, 2500.0),
         (0.9, 1.6, 4.0, 0.42, 60.0, 200.0, 250.0, 1800.0, 2500.0)]


def plan(T, nxt, prv):
    ops = []
    cnt = {"d": 0, "r": 0}
    tag = {}

    def add(eng, fn, rd, wr, cost, kind="c", sem=None, n=1, after=None, nbytes=0):
        ops.append({"eng": eng, "fn": fn, "rd": rd, "wr": wr, "cost": cost, "kind": kind, "sem": sem, "n": n,
                    "after": after, "also": set(), "bytes": nbytes})
        return len(ops) - 1

    def ap(r):
        return T[r[0]][:, r[1]:r[2]] if len(r) == 3 else T[r[0]][:, r[1]:r[2]:r[3]]

    def width(r):
        return r[2] - r[1] if len(r) == 3 else len(range(r[1], r[2], r[3]))

    def two(*rs):
        return all(SCRATCH[r[0]][2] in (BF, U16) for r in rs)

    def ind(win, lst):
        return ap(win).indirect(ap(lst))

    def cy(n, c):
        return ("c", max(64, n * c))

    def dma(eng, out, in_, rd, wr, nbytes, after=None, **kw):
        s = "d%d" % cnt["d"]
        cnt["d"] += 1
        return add(eng, lambda q: q.dma_start(out, in_, **kw), rd, wr, ("n", 1000.0 if eng == "g" else 60.0), "dma", s, 16, after, nbytes)

    def memset(o, v):
        add("v", lambda q: q.memset(ap(o), v), [], [o], cy(width(o), 0.5 if two(o) else 1))

    def copy(o, i):
        add("v", lambda q: q.tensor_copy(ap(o), ap(i)), [i], [o], cy(width(o), 0.5 if two(o, i) else 1))

    def tt(o, a, b, op):
        ps = SCRATCH[a[0]][0] == "psum" or SCRATCH[b[0]][0] == "psum"
        add("v", lambda q: q.tensor_tensor(ap(o), ap(a), ap(b), op), [a, b], [o], cy(width(o), 1 if ps else 2))

    def ts(o, i, s1, s2, op0, op1=None):
        rd = [i] + [s for s in (s1, s2) if isinstance(s, tuple)]
        a1 = ap(s1) if isinstance(s1, tuple) else s1
        a2 = ap(s2) if isinstance(s2, tuple) else s2
        if op1 is None:
            fn = lambda q: q.tensor_scalar(ap(o), ap(i), a1, None, op0)
        else:
            fn = lambda q: q.tensor_scalar(ap(o), ap(i), a1, a2, op0, op1)
        add("v", fn, rd, [o], cy(width(o), 0.5 if two(o, i) else 1))

    def gtt(o, win, lst, b, op):
        return add("v", lambda q: q.tensor_tensor(ap(o), ind(win, lst), ap(b), op), [win, lst, b], [o], ("g", width(o)))

    def scatter(win, lst, src, more=None):
        if more is None:
            return add("v", lambda q: q.tensor_copy(ind(win, lst), ap(src)), [lst, src], [win], ("s", width(src)))
        return add("v", lambda q: q.tensor_tensor(ind(win, lst), ap(src), ap(more), ALU.add), [lst, src, more], [win], ("s", width(src)))

    def act(o, i, func=ACT.Identity, bias=0.0, scale=1.0):
        return add("a", lambda q: q.activation(ap(o), ap(i), func, bias, scale), [i], [o], cy(width(o), 1))

    def affine(eng, o, i, scale, bias):
        if eng == "v":
            ts(o, i, scale, bias, ALU.mult, ALU.add)
        else:
            act(o, i, ACT.Identity, bias, scale)

    def gact(o, win, lst, bias=0.0, scale=1.0):
        return add("a", lambda q: q.activation(ap(o), ind(win, lst), ACT.Identity, bias, scale), [win, lst], [o], ("g", width(o)))

    def mm(o, terms, fresh=True, done=True):
        def fn(q):
            ins = None
            for k, (l, r) in enumerate(terms):
                ins = q.matmul(ap(o), ap(l), ap(r), fresh and k == 0, done and k == len(terms) - 1)
            return ins
        rd = []
        for l, r in terms:
            rd += [l, r]
        add("p", fn, rd, [o], ("p", len(terms) * max(64, width(o))))

    def z(s, i):
        return ("ZB", s * ZW + 15 - i, s * ZW + 143 - i)

    def wrap(s, name, c0, n):
        return [(z(s, i), (name, c0 + i, c0 + n, 16)) for i in range(16)]

    def sel(o, pattern, op, fill, base, cm):
        return add("g", lambda q: q.affine_select(ap(o), ap(o), pattern, op, fill, base, cm), [o], [o], ("n", 200.0 + 2 * width(o)))

    def iota(o, pattern, base, cm):
        if SCRATCH[o[0]][2] == I32:
            fn = lambda q: q.iota(ap(o), pattern, base, cm)
        else:
            fn = lambda q: q.iota(ap(o), pattern, base, cm, allow_small_or_imprecise_dtypes=True)
        add("g", fn, [], [o], ("n", 160.0 + 2 * width(o)))

    def send(srcs, dst, to, op=1, after=None):
        k = cnt["r"]
        cnt["r"] += 1
        rid, pid, mask, ne = to
        arr, out = "arr%d" % k, "out%d" % k
        if len(srcs) == 1:
            fn = lambda q: q.remote_dma(ap(dst), ap(srcs[0]), T.sem[arr], T.sem[out], pid, rid, mask)
        else:
            fn = lambda q: q.remote_dma_fused([RemoteDMATransfer(
                dst_ids=[DstId(rid=rid, pnc=pid)], dma_engine_mask=mask, remote_sem=T.sem[arr],
                srcs=[ap(s) for s in srcs], dsts=[ap(dst)], alu_op=op)], local_sem=T.sem[out])
        i = add("g", fn, list(srcs), [], ("n", 600.0 if k else 2000.0), "send", out, ne, after,
                (256 if two(dst) else 512) * width(dst) * len(srcs))
        add("n", None, [], [dst], ("n", 0.0), "arrive", arr, ne, after=i)
        return i

    XW, TW = ("X", 0, W), ("TB", 0, W)
    MI = ("MI", 0, 128)

    def load(name, src, c0, c1, after):
        return dma("s", T[name][:, c0:c1], src[:, c0:c1], [], [(name, c0, c1)], 256 * (c1 - c0), after)
    i = dma("s", T.NXI[:], T.nx[:], [], [("NXI", 0, 512)], 1 << 18)
    j = dma("a", T.PIN[:], T.pin[:], [], [("PIN", 0, 128)], 1 << 16)
    for k in range(OPT["pre"]):
        i = load("X", T.x, 2048 * k, 2048 * (k + 1), i)
    fill = OPT["fill"]
    memset(("TB", 0, 1024), 1.0)
    for k in range(fill):
        ops[act(("TB", 1024 * (k + 1), 1024 * (k + 2)), ("TB", 0, 1024))]["after"] = j
    memset(("TB", 1024 * (fill + 1), W), 1.0)
    copy(("NXH", 0, 512), ("NXI", 0, 512))
    tt(("NXL", 0, 512), ("NXI", 0, 512), ("NXH", 0, 512), ALU.subtract)
    i = dma("s", T.TB[0:128:16, 0:W], T.NXH[:], [("NXH", 0, 512)], [("TBm", 0, W)], 1 << 17, i)
    i = dma("s", T.TB[1:128:16, 0:W], T.NXL[:], [("NXL", 0, 512)], [("TBm", 0, W)], 1 << 17, i)
    i = dma("s", T.THI[:], T.th[:], [], [("THI", 0, 128)], 1 << 16, i)
    i = load("QR", T.q, 0, CS, i)
    for k in range(OPT["pre"], 4):
        i = load("X", T.x, 2048 * k, 2048 * (k + 1), i)
    i = load("QR", T.q, CS, R, i)
    copy(("LP", 0, 128), ("PIN", 0, 128))

    memset(MI, 1.0)
    j = sel(MI, [[-1, 128]], ALU.is_equal, 0.0, 0, 1)
    dma("g", T.CUI[:], T.cu[:], [], [("CUI", 0, 16)], 1 << 13, j)
    send([("PIN", 0, 128)], ("OP", 0, 128), nxt)
    memset(("MBN", 0, 128), 1.0)
    memset(("MBN", 128, 256), -1.0)
    sel(("MBN", 0, 256), [[0, 2], [-16, 8], [0, 16]], ALU.is_ge, 0.0, 0, 1)
    sel(("MBN", 0, 256), [[0, 2], [16, 8], [0, 16]], ALU.is_ge, 0.0, 15, -1)
    sel(("MBN", 128, 256), [[-1, 128]], ALU.is_ge, 0.0, 0, 1)
    sel(("MBN", 128, 256), [[-1, 128]], ALU.not_equal, -4096.0, 0, 1)

    def row(r):
        return ("MI", r, 128, 16)

    def zc(s):
        return ("ZB", s * ZW + 15, s * ZW + 143, 16)
    memset(("ZB", 0, NZ * ZW), 0.0)
    tt(zc(Z_L), row(0), row(1), ALU.add)
    ts(zc(Z_V), row(5), -16384.0, None, ALU.mult)
    tt(zc(Z_V), zc(Z_V), zc(Z_L), ALU.add)
    ts(zc(Z_K), row(2), -32768.0, None, ALU.mult)
    tt(zc(Z_K), zc(Z_K), row(3), ALU.add)
    tt(zc(Z_K), zc(Z_K), row(4), ALU.add)
    for s, v in ((Z_Q, -32768.0), (Z_M, 65536.0), (Z_S, 1.0)):
        ts(zc(s), ("MBN", 0, 128, 16), v, None, ALU.mult)
    MPc, MPn, MPm, MPf = [("MP", 128 * k, 128 * (k + 1)) for k in range(4)]
    memset(("MP", 0, 512), 0.0)
    for m0, m1, dst, src, v in ((0, 2, 5, 5, 1.0), (1, 3, 0, 0, 1.0), (1, 3, 1, 1, 1.0), (0, 1, 3, 3, 1.0), (0, 1, 4, 4, 1.0),
                                (0, 1, 2, 5, 4.0), (1, 2, 2, 5, -3072.0), (3, 4, 3, 0, 1.0), (3, 4, 4, 1, 1.0)):
        sel(("MP", 128 * m0 + dst, 128 * m1, 16), [[0, m1 - m0], [-16, 8]], ALU.not_equal, v, -src, 1)

    iota(("PI0", 0, 1), [[0, 1]], 0, 1)
    ts(("PI1", 0, 1), ("PI0", 0, 1), 15, None, ALU.bitwise_and)
    copy(("RC", 0, 1), ("PI1", 0, 1))
    ts(("RD", 0, 1), ("PI1", 0, 1), 512.0, None, ALU.mult)
    iota(("IDL", 0, 512), [[0, 8], [1, 64]], 0, 0)
    iota(("IDA", 0, 512), [[64, 8], [0, 64]], 0, 0)
    ts(("IDH", 0, 512), ("IDA", 0, 512), ("RD", 0, 1), None, ALU.add)
    iota(("I16", 0, 48), [[16, 48]], 832 - 4095, 0)
    ts(("TT", 0, 48), ("I16", 0, 48), ("RC", 0, 1), None, ALU.add)
    ts(("REP", 0, 16), ("I16", 0, 16), 0.0, ("RC", 0, 1), ALU.mult, ALU.add)
    iota(("FI0", 0, 80), [[1, 80]], 0, 80)
    ts(("FI1", 0, 80), ("FI0", 0, 80), 255, None, ALU.bitwise_and)
    ts(("FI", 0, 80), ("FI1", 0, 80), float(W), None, ALU.add)
    for k in range(4):
        dma("s", T.FI[k:128:16, 0:80], T.fr[:, 80 * k:80 * (k + 1)], [], [("FIm", 0, 80)], 2560, i)
    copy(("FH", 0, 80), ("FI", 0, 80))
    tt(("FL", 0, 80), ("FI", 0, 80), ("FH", 0, 80), ALU.subtract)
    memset(("FLB", 0, 320), 1.0)
    memset(("FLB", 320, 1024), 0.0)
    dma("s", T.FLB[0:128:16, 0:1280], T.FH[:], [("FH", 0, 80)], [("FLBm", 0, FLW)], 20480)
    dma("s", T.FLB[1:128:16, 0:1280], T.FL[:], [("FL", 0, 80)], [("FLBm", 0, FLW)], 20480)
    ts(("TH", 0, 128), ("THI", 0, 128), 32768.0, None, ALU.mult)
    iota(("CH", 0, 3 * CW), [[-8192, 3], [0, CW]], -8192, 0)
    copy(("LW", 0, 16), ("CUI", 0, 16))
    memset(("H", 0, 16), -1.0)
    memset(("M192", 0, 256), -192.0)
    memset(("BC", 0, 1), 64.0 + 256.0 + 4095.0)
    for a in range(NCH):
        va = ("V", a * CS, (a + 1) * CS)
        if OPT["init"][a] == "d":
            memset(va, A_OFF[0])
            dma("g", ap(va), T.q[:, a * CS:(a + 1) * CS], [va, ("X", W - 8, W)], [va], 512 * CS, accum_op=ALU.add)
        else:
            affine(OPT["init"][a], va, ("QR", a * CS, (a + 1) * CS), 1.0, A_OFF[0])
    for k in range(0, 16, 4):
        mm(("PW", 0, 512), [(z(Z_S, m), ("X", 512 * m, 512 * (m + 1))) for m in range(k, k + 4)], k == 0, k == 12)
    act(("SXS", 0, 512), ("PW", 0, 512))

    for p in range(PH):
        last = p == PH - 1

        def lst(h, a):
            return ("LP", 128 * p + CW * a, 128 * p + CW * (a + 1)) if h == 0 else ("LN", 128 * (h - 1) + CW * a, 128 * (h - 1) + CW * (a + 1))

        def run(name, a, k=p):
            return (name, k * R + a * CS, k * R + (a + 1) * CS)

        def fixed(h, a):
            return [(MI, ("CH", CW * (h - 1), CW * h))] + ([] if last else [(MI, ("TH", CW * a, CW * (a + 1)))])

        if p > 0:
            for a in range(NCH):
                affine(OPT["conv"].get((p, a), "v"), run("QR", a), run("V", a), 0.5 ** p, -A_OFF[p])
        if last:
            act(("QF", 0, CS), run("QR", NCH - 1), ACT.Identity, 257.5)
        for h in range(3):
            for a in range(NCH):
                if (p, h, a) in OPT["gv"]:
                    add("v", lambda q, o=run("G", a, h), l=lst(h, a): q.tensor_copy(ap(o), ind(TW, l)),
                        [TW, lst(h, a)], [run("G", a, h)], ("g", CS))
                else:
                    tag["G", p, h, a] = gact(run("G", a, h), TW, lst(h, a))
                mm(("PL%d" % a, 0, CW), wrap(Z_L, "G", h * R + a * CS, CS))
                copy(lst(h + 1, a), ("PL%d" % a, 0, CW))
        for a in range(NCH):
            hops = OPT["hops"].get((p, a), (1, 2, 3))

            def key(h, a):
                return (("PA%d", "PB%d", "PA%d")[hops.index(h)] % a, 0, CW)
            for h in hops:
                m0 = (h - 1) * R + a * CS
                mn, df = run("MN", a, h - 1), run("DF", a, h - 1)
                if p == 0 or h == 3:
                    tag["X", p, h, a] = gtt(df, XW, lst(h, a), run("QR", a), ALU.subtract)
                    mm(key(h, a), fixed(h, a) + wrap(Z_L, "G", m0, CS), True, False)
                    if (p, h, a) in OPT["neg"]:
                        ts(mn, df, 0.0, None, ALU.min)
                        mm(key(h, a), wrap(Z_Q, "DF", m0, CS), False, False)
                        mm(key(h, a), wrap(Z_M, "MN", m0, CS), False)
                    else:
                        act(mn, df, ACT.Abs)
                        mm(key(h, a), wrap(Z_Q, "MN", m0, CS), False)
                else:
                    tag["X", p, h, a] = gtt(mn, XW, lst(h, a), run("QR", a), ALU.min)
                    parts = [wrap(Z_K, "G", h * R + a * CS, CS), wrap(Z_Q, "QR", p * R + a * CS, CS)]
                    if h == 2:
                        parts.reverse()
                    mm(key(h, a), fixed(h, a) + parts[0], True, False)
                    mm(key(h, a), parts[1], False, False)
                    mm(key(h, a), wrap(Z_M, "MN", m0, CS), False)
                cw = (CW * a, CW * (a + 1))
                if h == hops[0]:
                    act(("K1S",) + cw, key(h, a))
                elif h == hops[1]:
                    tt(("M1",) + cw, ("K1S",) + cw, key(h, a), ALU.max)
            m2 = ("M2", 128 * p + cw[0], 128 * p + cw[1])
            tt(m2, ("M1",) + cw, key(hops[2], a), ALU.max)
            pn = ("A", 256 * p + cw[0], 256 * p + cw[1])
            ts(pn, m2, W - 1, None, ALU.bitwise_and)
            l0 = 128 * (p + 1) + cw[0]
            copy(("LP", l0, l0 + CW), pn)
            if not last:
                xg, lp = run("XG", a), ("LP", l0, l0 + CW)
                if OPT["xg"].get((p, a), "a") == "a":
                    tag["XG", p, a] = gact(xg, XW, lp, C_OFF * 2.0 ** p, 2.0 ** p)
                else:
                    tag["XG", p, a] = add("v", lambda q, xg=xg, lp=lp, s=2.0 ** p: q.tensor_scalar(
                        ap(xg), ind(XW, lp), C_OFF, s, ALU.add, ALU.mult), [XW, lp], [xg], ("g", CS))
                send([run("V", a), xg], run("V", a, p + 1), nxt)
                continue
            for c0 in range(0, CS, 512):
                s0 = a * CS + c0
                lp = ("LP", l0 + c0 // 16, l0 + c0 // 16 + 32)
                df, yq = ("DF", s0, s0 + 512), ("YQ", s0, s0 + 512)
                if a == NCH - 1:
                    tag["Y", p, c0] = gtt(df, XW, lp, ("QF", c0, c0 + 512), ALU.add)
                    ts(yq, df, 0.5, -129.0, ALU.mult, ALU.add)
                else:
                    xg, ps = ("XG", p * R + s0, p * R + s0 + 512), (("PL0", "PB0")[c0 // 512], 0, 512)
                    gact(xg, XW, lp, -0.5)
                    mm(ps, [(MI, xg), (MI, ("QR", p * R + s0, p * R + s0 + 512))])
                    act(df, ps, ACT.Identity, 192.0, 0.5)
                    act(yq, df, ACT.Identity, -192.0)
                dma("s", T.yq[:, s0:s0 + 512], ap(yq), [yq], [], 1 << 17)
        if last:
            copy(("YP", 0, 128), ("A", 256 * p, 256 * p + 128))
            dma("a", T.yp[:], T.YP[:], [("YP", 0, 128)], [], 1 << 16)
        else:
            send([("M2", 128 * p, 128 * (p + 1)), ("OP", 128 * p, 128 * (p + 1))], ("A", 256 * p + 128, 256 * (p + 1)), prv, 2)
            if p < PH - 2:
                send([("A", 256 * p, 256 * p + 128)], ("OP", 128 * (p + 1), 128 * (p + 2)), nxt)

        b = 64 * p
        fl = ("FLB", 256 * p, 256 * (p + 1))
        gc, gn = ("GC", 256 * p, 256 * (p + 1)), ("GN", 0, 256)
        c_, n_, t_, f_, c2 = [("FW", b + 16 * k, b + 16 * (k + 1)) for k in range(5)]
        lt, lf = ("LW", b + 32, b + 48), ("LW", b + 48, b + 64)
        if p == 0:
            for r, name in ((3, "IDH"), (4, "IDL")):
                dma("s", T.TB[r:128:16, 0:W], T[name][:], [(name, 0, 512)], [("TBm", 0, W)], 1 << 17, i)
        gact(gc, TW, ("LW", b, b + 16))
        mm(("PN", 0, 16), wrap(Z_L, "GC", 256 * p, 256))
        copy(("LW", b + 16, b + 32), ("PN", 0, 16))
        if not last:
            act(n_, ("PN", 0, 16))
        mm(("PW", 16, 32), wrap(Z_L, "FLB", 256 * p, 256))
        if p == 0:
            lt, lf = ("LW", 0, 16), ("LW", 64, 80)
            copy(lf, ("PW", 16, 32))
            act(c2, ("PW", 16, 32))
        else:
            mm(("PW", 0, 16), wrap(Z_V, "FLB", 256 * p, 256))
            act(f_, ("PW", 16, 32))
            tt(t_, c_, ("PW", 0, 16), ALU.max)
            if not last:
                act(("H", 16 * p, 16 * (p + 1)), ("PW", 0, 16), ACT.Sign)
                tt(("T1", 0, 16), c_, t_, ALU.subtract)
                tt(c2, ("T1", 0, 16), ("PW", 16, 32), ALU.add)
            e = b + (64 if last else 80)
            copy(("LW", b + 32, e), ("FW", b + 32, e))
        gact(gn, TW, ("LW", b + 16, b + 32))
        if p == 0:
            dma("s", T.TB[2:128:16, 0:W], T.SXS[:], [("SXS", 0, 512)], [("TBm", 0, W)], 1 << 17)
        if last:
            mm(("PN", 256, 512), [(z(Z_L, 0), fl)])
            mm(("PN", 0, 256), [(z(Z_L, 0), gn)])
            act(("NC", 0, 512), ("PN", 0, 512))
            tag["Tc", p] = scatter(("TO", 0, WT), lt, ("NC", 256, 512))
            tag["Tf", p] = scatter(("TO", 0, WT), lf, ("NC", 0, 256))
            dma("s", T.yn[:], T.TO[0:128:16, 0:W], [("TO", 0, W)], [("YN", 0, 1)], 1 << 18)
            break
        gact(("XCN", 0, 512), XW, ("LW", b, b + 32), -0.125, 0.5)
        mm(("PN", 256, 512), [(MI, ("XCN", 0, 256)), (MI, ("XCN", 256, 512))])
        act(("XF", 0, 256), ("PN", 256, 512), ACT.Identity, 192.0)
        mm(("PN", 256, 512), [(MPc, gc), (MPm, fl)] + 2 * [(z(Z_S, 2), ("XCN", 0, 256))])
        mm(("PN", 0, 256), [(MPn, gn), (MPf, fl), (z(Z_S, 2), ("XF", 0, 256))])
        act(("NCS", 0, 512), ("PN", 0, 512))
        tag["Tc", p] = scatter(("TB", 0, WT), lt, ("NCS", 256, 512))
        tag["Tf", p] = scatter(("TB", 0, WT), lf, ("NCS", 0, 256))
        tag["Xf", p] = scatter(("X", 0, WT), lf, ("XF", 0, 256), ("M192", 0, 256))
        if p == PH - 2:
            dma("g", T.TO[0:128:16, 0:W], T.TB[0:128:16, 0:W], [TW], [("TO", 0, W)], 1 << 18)
            dma("g", T.TO[0:128:16, 0:W], T.TB[1:128:16, 0:W], [TW], [("TO", 0, W)], 1 << 19, accum_op=ALU.add, max_dma_last_dim=4096)

        n = 16 * (p + 1)
        for k in range(p + 1):
            tag["E", p, k] = gtt(("E", 256 * k, 256 * (k + 1)), ("FW", 64 * k + 16, 64 * k + 32), ("REP", 0, 16), ("A", 256 * p, 256 * (p + 1)), ALU.is_equal)
            terms = [(MI, ("E", 256 * k + 16 * s, 256 * k + 16 * (s + 1))) for s in range(16)] + [(MI, ("H", 16 * k, 16 * (k + 1)))]
            terms += [(MI, ("U", 48 * m + 16 * k, 48 * m + 16 * (k + 1))) for m in range(k, p)]
            mm(("PW", 32 + 16 * k, 48 + 16 * k), terms)
        u = ("U", 48 * p, 48 * p + n)
        act(u, ("PW", 32, 32 + n), ACT.Relu, 0.0, -1.0)
        add("v", lambda q, u=u, n=n: q.tensor_tensor_scan(T.S[:, 0:n], ap(u), ap(u), 0.0, ALU.add, ALU.max), [u], [("S", 0, n)], cy(n, 1))
        mm(("PW", 80, 80 + n), [(("MBN", 0, 128), ("S", 0, n)), (("MBN", 128, 256), u)])
        if p < PH - 2:
            mm(("PW", 384, 385), [(("MBN", 0, 128), ("S", n - 1, n))])
        tt(("TM", 0, n), ("TT", 0, n), ("PW", 80, 80 + n), ALU.min)
        bc = ("BC", 8 * p, 8 * p + 1)
        ts(("TG", 0, n), ("TM", 0, n), bc, None, ALU.add)
        if p < PH - 2:
            ts(("BC", 8 * p + 8, 8 * p + 9), ("PW", 384, 385), bc, 256.0 * (p + 2) + 4095.0, ALU.add, ALU.max)
        tag["F", p] = scatter(("FLB", 0, FLW), ("TG", 0, n), ("GC", 0, 16 * n))
    for chain in chains():
        chain = [tag[t] for t in chain if t in tag]
        for u0, u1 in zip(chain, chain[1:]):
            ops[u1]["also"].add(u0)
    return ops


def chains():
    seq = []
    for p in range(PH):
        for t in OPT["vseq"][min(p, 1)]:
            if t[0] == "X":
                seq.append(("X", p, OPT["hops"].get((p, t[2]), (1, 2, 3))[t[1]], t[2]))
            elif t[0] == "E":
                seq += [("E", p - 1, k) for k in range(p)]
            elif t[0] == "XG":
                seq.append(("XG", p, 1))
            elif t[0] == "F":
                seq.append(("F", p - 1))
            else:
                seq.append((t[0], p))
    return [seq, [("G", 0, 0, 0), ("G", 0, 0, 1)], [("Tc", PH - 1), ("Tf", PH - 1), ("Y", PH - 1, 0)]]


def depend(ops):
    hist = {}
    deps = []
    for i, o in enumerate(ops):
        d = set()
        for r, w in [(r, False) for r in o["rd"]] + [(r, True) for r in o["wr"]]:
            name, lo, hi = r[0], r[1], r[2]
            part = name not in SCRATCH and name.endswith("m")
            if part:
                name = name[:-1]
            psum = name in SCRATCH and SCRATCH[name][0] == "psum"
            for (j, l2, h2, w2, p2) in hist.get(name, []):
                if j == i:
                    continue
                if psum:
                    if ops[j]["eng"] != o["eng"] or (w and l2 < hi and lo < h2):
                        d.add(j)
                elif (w or w2) and l2 < hi and lo < h2 and not (part and p2):
                    d.add(j)
            hist.setdefault(name, []).append((i, lo, hi, w, part))
        deps.append(d)
    reach = []
    for i, d in enumerate(deps):
        far = set()
        for j in d:
            far |= reach[j]
        reach.append(far | d)
        deps[i] = sorted(d - far)
    return deps


def timer(ops, deps, par):
    cyc, ga, sc, pc, fix, hop, bw, dl, rl = par
    k = {"c": cyc, "g": cyc * ga, "s": cyc * sc, "p": pc}
    dur = [o["cost"][1] if o["cost"][0] == "n" else fix + k[o["cost"][0]] * o["cost"][1] for o in ops]
    lat = [{"c": 0.0, "dma": dl, "send": rl, "arrive": 200.0}[o["kind"]] for o in ops]
    bt = [o["bytes"] / bw for o in ops]
    n = len(ops)
    eng = ["vapgsn".index(o["eng"]) for o in ops]
    dd = [list(deps[i]) + ([o["after"]] if o["kind"] == "arrive" else []) for i, o in enumerate(ops)]

    row = [(eng[i], dd[i], dur[i], bt[i], lat[i] + (0.0 if bt[i] else hop)) for i in range(n)]

    def walk(order, end, free, tail):
        far, both, bus = 0.0, 0.0, free[6]
        for i in order:
            e, d, u, b, l = row[i]
            t = free[e]
            for j in d:
                if end[j] > t:
                    t = end[j]
            both += t
            t += u
            free[e] = t
            t += l
            if b:
                bus = (bus if bus > t else t) + b
                t = bus + hop
            end[i] = t
            t += tail[i]
            if t > far:
                far = t
        free[6] = bus
        return far, both

    def run(order):
        end = [0.0] * n
        far = walk(order, end, [0.0] * 7, [0.0] * n)[0]
        start, free = [0.0] * n, [0.0] * 6
        for i in order:
            start[i] = max([free[eng[i]]] + [end[j] for j in dd[i]])
            free[eng[i]] = start[i] + dur[i]
        return far, start

    def part(order, lo, hi):
        tail, rest = [0.0] * n, [0.0] * 7
        for i in reversed(order[hi:]):
            e, d, u, b, l = row[i]
            t = tail[i]
            if b:
                t = rest[6] = b + max(t + hop, rest[6])
            t = rest[e] = u + max(l + t, rest[e])
            for j in d:
                if t > tail[j]:
                    tail[j] = t
        end, free0 = [0.0] * n, [0.0] * 7
        base = walk(order[:lo], end, free0, tail)[0]

        def time(stretch):
            free = free0[:]
            far, both = walk(stretch, end, free, tail)
            return max(base, far, max([free[e] + rest[e] for e in range(7)])), both
        return time
    return run, dur, [lat[i] + bt[i] + hop for i in range(n)], part


def arrange(ops, deps):
    n = len(ops)
    timers = [timer(ops, deps, par) for par in GUESS]
    runs = [t[0] for t in timers]
    dur, lag = timers[0][1:3]
    eng = [o["eng"] for o in ops]
    pre = [set(deps[i]) | o["also"] | ({o["after"]} if o["after"] is not None else set()) for i, o in enumerate(ops)]
    post = [set() for _ in range(n)]
    prio = [0.0] * n
    line, seen = [], set()
    while len(line) < n:
        for i in range(n):
            if i not in seen and pre[i] <= seen:
                seen.add(i)
                line.append(i)
    for i in reversed(line):
        prio[i] += dur[i] + lag[i]
        for j in pre[i]:
            post[j].add(i)
            queued = j not in deps[i] and ops[i]["kind"] != "arrive"
            prio[j] = max(prio[j], prio[i] - (lag[j] if queued else 0.0))
    prio = [prio[i] + (2000.0 if dur[i] < 400.0 else 0.0) for i in range(n)]
    left = [len(s) for s in pre]
    ready = [i for i in range(n) if not left[i]]
    rt, free, cur = [0.0] * n, {e: 0.0 for e in eng}, []
    while ready:
        t, e = min((max(free[eng[i]], rt[i]), eng[i]) for i in ready)
        i = max((k for k in ready if eng[k] == e and rt[k] <= t + 150.0), key=lambda k: prio[k])
        ready.remove(i)
        cur.append(i)
        t = max(t, rt[i])
        free[e] = t + dur[i]
        for u in post[i]:
            queued = i not in deps[u] and ops[u]["kind"] != "arrive"
            rt[u] = max(rt[u], t if queued else free[e] + lag[i])
            left[u] -= 1
            if not left[u]:
                ready.append(u)

    rng = np.random.RandomState(OPT["seed"])
    size, sweeps, moves = OPT["size"], OPT["sweeps"], OPT["moves"]
    best, bs = cur, 1e18
    for sweep in range(sweeps):
        heat = OPT["heat"] * (1.0 - sweep / sweeps) ** 2
        for lo in range(-int(rng.randint(0, size // 2)), n - size // 2, size // 2):
            start = runs[0](cur)[1]
            cur = sorted(cur, key=lambda k: start[k])
            lo, hi = max(lo, 0), min(lo + size, n)
            times = [t[3](cur, lo, hi) for t in timers]

            def score(o):
                t, both = times[0](o)
                return 2.0 * t + OPT["early"] * both / n + sum(f(o)[0] for f in times[1:])
            w, m = cur[lo:hi], hi - lo
            sc = score(w)
            pick, jump, side, luck = [x.tolist() for x in (rng.randint(0, m, moves), rng.geometric(0.45, moves),
                                                           rng.randint(0, 2, moves), rng.random_sample(moves))]
            for a, todo, up, lk in zip(pick, jump, side, luck):
                v = w[a]
                step, rel = (1, post) if up else (-1, pre)
                b, drag, block = a, [v], set(rel[v])
                while todo:
                    b += step
                    if b < 0 or b >= m:
                        break
                    u = w[b]
                    if u in block:
                        if eng[u] == eng[v] or len(drag) > 5:
                            break
                        drag.append(u)
                        block |= rel[u]
                    elif eng[u] == eng[v]:
                        todo -= 1
                if todo:
                    continue
                ds = set(drag)
                if step == 1:
                    new = w[:a] + [u for u in w[a:b + 1] if u not in ds] + drag + w[b + 1:]
                else:
                    new = w[:b] + drag[::-1] + [u for u in w[b:a + 1] if u not in ds] + w[a + 1:]
                s = score(new)
                if s <= sc or lk < math.exp((sc - s) / heat):
                    w, sc = new, s
            cur = cur[:lo] + w + cur[hi:]
        s = runs[0](cur)[0] + sum(r(cur)[0] for r in runs)
        if s < bs:
            best, bs = cur, s
    return best, [r(best)[0] for r in runs], runs[0](best)[1], dur


ORDER = []


def rank_program(g, core, T, topo):
    rank = T.rank_of(core)
    if rank is None:
        return
    N = len(T.cores)

    def way(dst):
        rid, pid, _ = topo.addr(dst)
        return rid, pid, topo.mask(core, dst), len(topo.engines(core, dst))

    ops = plan(T, way(T.cores[(rank + 1) % N]), way(T.cores[(rank - 1) % N]))
    deps = depend(ops)
    if not ORDER:
        ORDER.extend(arrange(ops, deps)[0])
    queue = {"v": g.vector, "a": g.scalar, "p": g.tensor, "g": g, "s": g.sync}
    count = {}
    mark = {}
    clock = {}
    known = {e: {} for e in queue}
    for i in ORDER:
        o = ops[i]
        e = o["eng"]
        s = o["sem"] or "e" + e
        count[s] = count.get(s, 0) + o["n"]
        mark[i] = (s, count[s])
        if e == "n":
            clock[i] = {s: count[s]}
            continue
        kn = known[e]
        for j in sorted(deps[i], key=lambda j: -mark[j][1]):
            if e == "p" and ops[j]["eng"] == "p":
                continue
            sj, cj = mark[j]
            if kn.get(sj, 0) < cj:
                queue[e].wait_ge(T.sem[sj], cj)
                for k, v in clock[j].items():
                    if kn.get(k, 0) < v:
                        kn[k] = v
        ins = o["fn"](queue[e])
        if o["kind"] != "send":
            ins.then_inc(T.sem[s], o["n"])
        clock[i] = dict(kn)
        clock[i][s] = count[s]
    for s, c in count.items():
        g.wait_ge(T.sem[s], c)
